import numpy as np, ml_dtypes
CORES = [1,5,17,21,33,37,49,53]
N = 8
import mx_ref
BF = ml_dtypes.bfloat16
def gcols(t, e):
    v = np.concatenate([t.reshape(8, 16, -1, 4), np.zeros((8, 16, 1, 4), BF)], axis=2)
    return np.ascontiguousarray(np.stack([v[g][:, e[g]] for g in range(8)])).reshape(128, -1)
def tile(rs):
    return np.stack(rs, axis=2).reshape(128, -1).astype(BF)
def pick(q, e):
    c = np.concatenate([q[0].reshape(128, -1, 4), np.zeros((128, 1, 4), np.uint8)], axis=1); s = np.concatenate([q[1], np.ones((16, 1), np.uint8)], axis=1)
    return (np.ascontiguousarray(c[:, e].reshape(128, -1)), np.ascontiguousarray(s[:, e]))
def join(*qs):
    return (np.concatenate([q[0] for q in qs], axis=1), np.concatenate([q[1] for q in qs], axis=1))
def put(q, e, v):
    c, s = q[0].reshape(128, -1, 4).copy(), q[1].copy(); c[:, e] = v[0].reshape(128, -1, 4); s[:, e] = v[1]
    return (c.reshape(128, -1), s)
def pk(c, s):
    return (np.ascontiguousarray(c), mx_ref.live(s))
def emit(q):
    return q[0], q[1]
def packed(v, rng):
    q = [mx_ref.quantize(np.ascontiguousarray(v[r])) for r in range(N)]
    return np.stack([a for a, b in q]), np.stack([mx_ref.plane(b, rng) for a, b in q])
def values_of_codes():
    e, c = np.zeros((128, 128, 4), np.float32), np.zeros((128, 2, 4), np.uint8)
    e[np.arange(128), np.arange(128), 0] = 1
    c[:127, :, 0] = np.arange(256).reshape(2, 128).T[:127]
    return mx_ref.matmul(mx_ref.quantize(e.reshape(128, 512).astype(BF)), (c.reshape(128, 8), np.full((16, 2), 127, np.uint8))).T.reshape(-1).astype(np.float64)
CODE_VALUE, SCALE_VALUE = values_of_codes(), 2.0 ** (np.arange(256) - 127.0)
def decode(q):
    return (CODE_VALUE[q[0]].reshape(16, 8, -1, 4) * SCALE_VALUE[q[1]][:, None, :, None] + 0.0).reshape(128, -1).astype(np.float32)
def f(rng, *shape):
    return mx_ref.flush((rng.standard_normal(shape, dtype=np.float32) * np.exp2(rng.integers(-2, 3, shape[:-1] + (1,)))).astype(BF))
def wide(rng, *shape, cols=0):
    v = rng.standard_normal(shape, dtype=np.float32) * np.exp2(rng.integers(-12, 13, shape)).astype(np.float32)
    if cols: v *= np.repeat(np.exp2(rng.integers(-cols, cols + 1, shape[:-2] + (1, shape[-1] // 4))) * (rng.random(shape[:-2] + (1, shape[-1] // 4)) > 0.0625), 4, axis=-1).astype(np.float32)
    return mx_ref.flush(v.astype(BF))
C, R = 512, 2
def order(p):
    return np.argsort(-(p[::16] + np.float32(0.0)), axis=1, kind="stable")
def clear(v):
    v = np.array(v)
    v[np.abs(v.astype(np.float32)) < np.float32(2.0 ** -16)] = 0
    return v
def numbers_of(rng):
    return {"x": clear(f(rng, N, 128, 4 * C)), "u": np.array(f(rng, N, 128, 512)), "v": np.array(f(rng, N, 128, 512))}
def weights(rng, w):
    c, p = packed(np.stack([w] * N), rng)
    return {"wc": c, "ws": p}
def aside(rng, k):
    w = np.array(f(rng, 128, 2048)).reshape(8, 16, 4, 8, 16, 4)
    w[:, :k] = 0
    w[:, :, :, :, 0] = 0
    w[:, :, :, :, 8:] = 0
    return weights(rng, w.reshape(128, 2048))
def signs(rng):
    return np.stack([rng.permutation(8) % 2 * 2.0 - 1.0 for r in range(N)])
def setup_inputs(rng):
    return {**numbers_of(rng), **weights(rng, f(rng, 128, 2048))}
def setup_inputs_ties(rng):
    d = numbers_of(rng)
    e = rng.permutation(N)
    x = d["x"].reshape(N, 8, 16, C, 4)
    for r in range(N):
        k = np.zeros(C, int) if r == e[0] else rng.permutation(C) % 3
        a = x[r][:, :8, :3].copy()
        a[:, :, 2] = 0
        x[r][:, :8] = a[:, :, k]
    x[e[1]] = 0
    u = d["u"].reshape(N, 8, 16, 128, 4)
    u[:, :, 8:, ::16] = 0
    w = np.array(f(rng, 128, 2048)).reshape(8, 16, 4, 8, 16, 4)
    w[:, 8:, :, :, :8] = 0
    return {"x": x.reshape(N, 128, 4 * C), "u": u.reshape(N, 128, 512), "v": d["v"], **weights(rng, w.reshape(128, 2048))}
def setup_inputs_near(rng):
    d = numbers_of(rng)
    x = d["x"].astype(np.float32).reshape(N, 8, 16, C, 4)
    s = (np.arange(C) // 2 + rng.integers(0, C // 2, (N, 8, 1))) % (C // 2)
    g = ((s[..., None] >> np.arange(8)) & 1) * np.exp2(np.arange(8) - 23.0)
    x[:, :, 0] = 0
    x[:, :, 0, :, 0] = signs(rng)[:, :, None]
    x[:, :, 8] = g[..., :4]
    x[:, :, 9] = g[..., 4:]
    x[:, :, 10:] = 0
    u = d["u"].reshape(N, 128, 128, 4)
    u[:, :, ::16] = 0
    k = np.where(rng.permutation(N) < N // 2, 2.0 ** -30, 1.0).astype(np.float32).astype(BF)
    for h in range(0, 128, 16):
        u[:, h, h, 0] = k
        u[:, h + 8:h + 10, h] = k[:, None, None]
    return {"x": x.reshape(N, 128, 4 * C).astype(BF), "u": u.reshape(N, 128, 512), "v": d["v"], **aside(rng, 0)}
def setup_inputs_huge(rng):
    d = numbers_of(rng)
    x = 2.0 ** 30 * (0.6 + 0.4 * rng.random((N, 128, C, 4)))
    c = np.stack([rng.permutation(C) % 2 * 2.0 - 1.0 for r in range(N)])
    c[rng.permutation(N) < N // 2] = 1
    x *= c[:, None, :, None]
    u = d["u"].reshape(N, 128, 128, 4)
    a = 2.0 ** 30 * (1 - 0.25 * rng.random((N, 128, 8, 4))) * signs(rng)[:, None, :, None]
    u[:, :, ::16] = a.astype(np.float32).astype(BF)
    w = np.zeros((128, 4, 128, 4), np.float32)
    i = np.arange(128)
    for b in range(4): w[i, b, i, b] = 16
    return {"x": x.astype(np.float32).reshape(N, 128, 4 * C).astype(BF), "u": u.reshape(N, 128, 512), "v": d["v"], **weights(rng, w.reshape(128, 2048).astype(BF))}
def setup_inputs_crowd(rng):
    d = numbers_of(rng)
    x = d["x"].astype(np.float32).reshape(N, 8, 16, C, 4)
    a, b = np.triu_indices(N, 1)
    k = rng.permutation(len(a))[(np.arange(C)[None, :] + np.arange(8)[:, None]) % len(a)]
    z = rng.integers(4, 8, (8, 8, C, 4)) * rng.choice([-1.0, 1.0], (8, 8, C, 4)) * 2.0 ** 26
    s = C - 1 - np.arange(C)
    digits = np.stack([s % 8, s // 8 % 8, s // 64, 0 * s], axis=1)
    for r in range(N):
        l = rng.integers(4, 8, (8, 8, C, 4)) * rng.choice([-1.0, 1.0], (8, 8, C, 4))
        l = np.where((a[k] == r)[:, None, :, None], z, np.where((b[k] == r)[:, None, :, None], -z, l))
        for g in range(8):
            o = rng.permutation(C)
            p = x[r, g]
            p[8:, o] = l[g]
            p[0, o] = digits
    u = d["u"].reshape(N, 128, 128, 4)
    u[:, :, ::16] = 0
    for h in range(0, 128, 16): u[:, h, h, :3] = np.array([1, 8, 64], np.float32).astype(BF)
    return {"x": x.reshape(N, 128, 4 * C).astype(BF), "u": u.reshape(N, 128, 512), "v": d["v"], **aside(rng, 8)}
def setup_inputs_spread(rng):
    d = setup_inputs(rng)
    d["x"] = clear(wide(rng, N, 128, 4 * C, cols=6))
    return d
def check_inputs(d):
    b = []
    for k in ("x", "u", "v"):
        a = np.abs(d[k].astype(np.float32))
        if not (np.isfinite(a).all() and ((a == 0) | (a >= 2.0 ** -30) & (a <= 2.0 ** 30)).all()): b.append("a value of " + k)
    if (d["wc"] != d["wc"][:1]).any(): b.append("wc differs between ranks")
    s = [mx_ref.live(p) for p in d["ws"]]
    if any((p != s[0]).any() for p in s): b.append("ws differs between ranks")
    if not (np.abs(decode(pk(d["wc"][0], d["ws"][0]))) <= 2.0 ** 30).all(): b.append("a number of W beyond 2**30")
    return b
def reference(x, u, v, wc, ws):
    w = pk(wc[0], ws[0])
    lay = [pick(w, np.arange(128 * b, 128 * b + 128)) for b in range(4)]
    qu = [mx_ref.quantize(u[r]) for r in range(N)]
    now = [x[r] for r in range(N)]
    for t in range(R):
        o = [order(mx_ref.matmul(qu[r], mx_ref.quantize(now[r]))) for r in range(N)]
        total = decode(mx_ref.quantize(gcols(now[0], o[0])))
        for r in range(1, N): total = total + decode(mx_ref.quantize(gcols(now[r], o[r])))
        m = mx_ref.quantize((total * np.float32(0.125)).astype(BF))
        h = mx_ref.quantize(tile([np.maximum(mx_ref.matmul(lay[b], m), np.float32(0.0)) * np.float32(0.0625) for b in range(4)]))
        back = decode(h).astype(BF)
        for r in range(N):
            i = np.argsort(o[r], axis=1)
            now[r] = ((now[r].astype(np.float32) + gcols(back, i).astype(np.float32)) * np.float32(0.5)).astype(BF)
    y, ol = np.zeros((N, 128, C), np.float32), np.zeros((N, 8, C), np.float32)
    oc, osc = np.zeros((N, 128, 4 * C), np.uint8), np.zeros((N, 16, C), np.uint8)
    for r in range(N):
        q = mx_ref.quantize(now[r])
        y[r] = mx_ref.matmul(mx_ref.quantize(v[r]), q)
        ol[r] = o[r]
        oc[r], osc[r] = emit(q)
    return {"y": y, "ol": ol, "oc": oc, "osc": osc}

@@ -1,0 +1,371 @@
+import numpy as np
+from concourse.bass import DstId, RemoteDMATransfer
+from concourse.mybir import dt, AluOpType as A, ActivationFunctionType as F
+
+R = 2
+C = 512
+BL = 64
+NS = [512, 448, 384, 320, 256, 192, 128, 128]
+CO = [sum(NS[:s]) for s in range(8)]
+FC = sum(NS)
+ROWS = [[-1, 31, 30, 29]] + [[32 - 4 * s - t for t in range(4)] for s in range(1, 8)]
+MINE = [1]
+BIG = 2.0 ** 94
+
+E4, U8, BF, F32, I32, U16 = "float8_e4m3fn_x4", "uint8", "bfloat16", "float32", "int32", "uint16"
+SCRATCH = {}
+
+
+def _sb(n, ty, *names):
+    for k in names: SCRATCH[k] = ("sbuf", [128, n], ty)
+
+
+def _mx(n, *pairs):
+    for a, b in pairs:
+        _sb(n, E4, a)
+        _sb(n, U8, b)
+
+
+_sb(2048, BF, "x0", "x1", "x2", "st", "sh", "sn", "eb", "junk")
+_sb(512, BF, "ut", "vt", "bt", "bt2", "eighth", "mt", "ht", "c0", "bm", "maskb", "rst", "hold", "hk0", "hk")
+_sb(4 * NS[1], BF, "sg")
+_sb(4 * FC, BF, "ft")
+_sb(512, F32, "iot", "pr", "pm", "sc", "cum", "e1", "e2", "inv", "olt", "yt")
+_sb(192, F32, "acb")
+_sb(32, F32, "m0", "ac0", "rs", "a1", "a2", "a2s", "a3")
+_sb(1, F32, "pi", "pi1", "p15", "scol", "isc", "isc4")
+_sb(1, I32, "p0", "p1")
+_sb(8, I32, "uo0")
+_sb(8, U16, "uoff")
+_sb(32, U16, "il", "l0", "l1", "l2", "l3")
+_mx(128, ("uq", "us"), ("ur", "urs"), ("vq", "vsc"), ("bq", "bs"), ("mq", "ms"), ("hq0", "hs0"), ("hq1", "hs1"))
+_mx(512, ("wq", "wsc"), ("eq", "es"), ("xq0", "xs0"), ("xq1", "xs1"), ("xq2", "xs2"), ("sq0", "ss0"), ("sq1", "ss1"), ("hl0", "hp0"), ("hl1", "hp1"))
+_mx(640, ("lc0", "ls0"), ("lc1", "ls1"))
+_mx(FC, ("fq", "fs"))
+SCRATCH.update({"pp": ("psum", [128, 512], F32), "pc": ("psum", [128, 512], F32), "pe": ("psum", [128, 512], F32), "pa": ("psum", [128, 2048], F32)})
+SEMAPHORES = ["vs", "ss", "ps", "gs", "lx", "lu", "lv", "lw", "lws", "lsem", "so", "sy"]
+SEMAPHORES += ["sa%d_%d" % (t, r) for t in range(R) for r in range(8)] + ["%s%d" % (k, t) for t in range(R) for k in ("ha", "cs", "ch")]
+
+
+def owners(T, topo):
+    by = {}
+    for r, c in enumerate(T.cores): by.setdefault(topo.chip(c), []).append(r)
+    first, second = [], []
+    for k, ch in enumerate(sorted(by)):
+        first.append(by[ch][k % 2])
+        second.append(by[ch][1 - k % 2])
+    return first + second
+
+
+def rank_program(g, core, T, topo):
+    rank = T.rank_of(core)
+    if rank is None: return
+    sem = T.sem
+    V, S, P, Y = g.vector, g.scalar, g.tensor, g.sync
+    Q = {"g": g, "v": V, "s": S, "p": P, "y": Y}
+    SEM = {"v": "vs", "s": "ss", "p": "ps", "g": "gs"}
+    cnt = {"vs": 0, "ss": 0, "ps": 0, "gs": 0}
+    seen = {q: {} for q in Q}
+
+    def need(q, *deps):
+        for d in deps:
+            if seen[q].get(d[0], 0) < d[1]:
+                Q[q].wait_ge(sem[d[0]], d[1])
+                seen[q][d[0]] = d[1]
+
+    def done(q, inst):
+        k = SEM[q]
+        inst.then_inc(sem[k], 1)
+        cnt[k] += 1
+        return (k, cnt[k])
+
+    def v(inst): return done("v", inst)
+    def s(inst): return done("s", inst)
+    def p(inst): return done("p", inst)
+    def gg(inst): return done("g", inst)
+
+    Y.dma_start(T.x0[:], T.x[:, :]).then_inc(sem.lx, 16)
+    S.dma_start(T.ut[:], T.u[:, :]).then_inc(sem.lu, 16)
+    Y.dma_start(T.wq[:].bitcast(dt.uint8), T.wc[:, :]).then_inc(sem.lw, 16)
+    Y.dma_start(T.wsc[:], T.ws[:, :]).then_inc(sem.lws, 16)
+    Y.dma_start(T.vt[:], T.v[:, :]).then_inc(sem.lv, 16)
+
+    small = {"allow_small_or_imprecise_dtypes": True}
+    k_p = gg(g.iota(T.p0[:], [[0, 1]], 0, 1))
+    k_uo = gg(g.iota(T.uo0[:], [[16, 8]], 0, 0))
+    k_c = gg(g.iota(T.c0[:], [[0, 32], [1, 16]], 0, 0, **small))
+    k_m = gg(g.iota(T.m0[:], [[16, 32]], 15, 0, **small))
+    c_8 = v(V.memset(T.eighth[:], 0.125))
+    need("g", c_8)
+    k_b0 = gg(g.affine_select(T.bt2[:], T.eighth[:], [[-16, 8], [0, 64]], A.is_ge, 0.0, 0, 1))
+    need("g", k_b0)
+    k_b1 = gg(g.affine_select(T.bt[:], T.bt2[:], [[16, 8], [0, 64]], A.is_ge, 0.0, 15, -1))
+    k_io = gg(g.iota(T.iot[:], [[1, 512]], 1, 0, **small))
+    for b in range(4):
+        k_eb = gg(g.affine_select(T.eb[:, 512 * b:512 * b + 512], T.eighth[:], [[-1, 512]], A.is_equal, 0.0, b, 4))
+    z = []
+    for i in range(8):
+        w = 64 if i < 7 else 128
+        z.append(v(V.memset(T.ft[:, 4 * (CO[i] + NS[i] - w):4 * (CO[i] + NS[i])], 0.0)))
+    c_rs = v(V.memset(T.rs[:], 0.0))
+    need("v", k_p)
+    c_p = v(V.tensor_scalar(T.p1[:], T.p0[:], 15, None, A.bitwise_and))
+    need("v", k_uo)
+    c_uoff = v(V.tensor_copy(T.uoff[:], T.uo0[:]))
+    need("v", c_p)
+    c_pi = v(V.tensor_copy(T.pi[:], T.p1[:]))
+    c_pi1 = v(V.tensor_scalar(T.pi1[:], T.p1[:], 1.0, None, A.add))
+    c_p15 = v(V.tensor_scalar(T.p15[:], T.p1[:], 15.0, None, A.is_equal))
+    need("v", k_c, c_pi)
+    c_bm = v(V.tensor_scalar(T.bm[:], T.c0[:], T.pi[:], None, A.not_equal))
+    need("s", c_bm)
+    c_mask = s(S.activation(T.maskb[:], T.bm[:], F.Copy, scale=-2.0 * BIG, bias=BIG))
+    c_hold = v(V.tensor_scalar(T.hold[:], T.c0[:], 1.0, None, A.min))
+    need("s", c_hold)
+    c_rst = s(S.activation(T.rst[:], T.hold[:], F.Copy, scale=2.0 * BIG, bias=-BIG))
+    need("v", ("lu", 16))
+    c_uq = v(V.quantize_mx(T.uq[:], T.us[:], T.ut[:]))
+    need("v", c_uq, c_uoff)
+    c_ur = v(V.tensor_copy(T.ur[:, 0:128].bitcast(dt.uint32), T.uq[:, 0:128].bitcast(dt.uint32).indirect(T.uoff[:, 0:8])))
+    need("s", c_uq)
+    c_urs = s(S.activation(T.urs[:, 0:128], T.us[:, 0:128].indirect(T.uoff[:, 0:8]), F.Copy))
+    c_hk0 = v(V.tensor_scalar(T.hk0[:], T.c0[:], T.pi1[:], 1024.0, A.is_equal, A.mult))
+    need("v", ("lx", 16))
+    xq = v(V.quantize_mx(T.xq0[:], T.xs0[:], T.x0[:]))
+    need("v", c_hk0)
+    c_hk = v(V.tensor_tensor(T.hk[:], T.hk0[:], T.bm[:], A.max))
+    c_sc = v(V.tensor_scalar(T.scol[:], T.p15[:], -127.875, 128.0, A.mult, A.add))
+    c_isc = v(V.tensor_scalar(T.isc[:], T.p15[:], 8.0 - 2.0 ** -7, 2.0 ** -7, A.mult, A.add))
+    c_isc4 = v(V.tensor_scalar(T.isc4[:], T.p15[:], 4.0 - 2.0 ** -8, 2.0 ** -8, A.mult, A.add))
+    need("v", k_m)
+    c_ac0 = v(V.tensor_scalar(T.ac0[:], T.m0[:], T.pi[:], None, A.subtract))
+
+    ow = owners(T, topo)
+    own = ow.index(rank)
+    mate = [r for r in range(len(T.cores)) if r != rank and topo.chip(T.cores[r]) == topo.chip(core)]
+    far = [r for r in range(len(T.cores)) if topo.chip(T.cores[r]) != topo.chip(core)]
+    fe = topo.engines(core, T.cores[far[0]])
+    pairs = [fe[2 * k:2 * k + 2] for k in range(4)]
+    ne = [e for e in topo.engines(core, T.cores[mate[0]]) if e not in fe][:4]
+    local = [0]
+
+    def put(src, rs, dst, sm, es):
+        ids = []
+        for r in rs:
+            rid, pid, _se = topo.addr(T.cores[r])
+            ids.append(DstId(rid=rid, pnc=pid))
+        local[0] += len(es)
+        return RemoteDMATransfer(dst_ids=ids, dma_engine_mask=sum(1 << e for e in es), remote_sem=sem[sm], srcs=[src], dsts=[dst] * len(rs))
+
+    TURN = [([0, 1, 2], [3, 0, 1]), ([3, 2, 0], [1, 2, 3])]
+
+    def quantise_flags(i, d):
+        need("v", d)
+        a, b = CO[i], CO[i] + NS[i]
+        return v(V.quantize_mx(T.fq[:, a:b], T.fs[:, a:b], T.ft[:, 4 * a:4 * b]))
+
+    jd = []
+    for t in range(R):
+        X, XN = T["x%d" % t], T["x%d" % (t + 1)]
+        XQ, XS = T["xq%d" % t], T["xs%d" % t]
+        SQ, SS, LC, LS = T["sq%d" % t], T["ss%d" % t], T["lc%d" % t], T["ls%d" % t]
+        HQ, HS, HL, HP = T["hq%d" % t], T["hs%d" % t], T["hl%d" % t], T["hp%d" % t]
+        last = t == R - 1
+        need("p", xq, c_ur, c_urs)
+        d_p = p(P.matmul_mx(T.pp[:], T.ur[:], T.urs[:], XQ[:], XS[:], True, True))
+        need("v", d_p, c_mask)
+        d_pm = v(V.tensor_tensor(T.pm[:], T.pp[:], T.maskb[:], A.min))
+        need("s", d_pm)
+        d_pr = s(S.activation(T.pr[:], T.pp[:], F.Copy))
+        need("v", d_pm, c_rst)
+        d_sc = v(V.tensor_tensor_scan(T.sc[:], T.rst[:], T.pm[:], -BIG, A.min, A.max))
+        need("s", d_sc, c_rs, z[-1], d_pr)
+        own_q = {}
+        for i in MINE:
+            f0, sg = 4 * CO[i], []
+            for j in range(5):
+                if j < 4:
+                    m = ROWS[i][j]
+                    sg.append(s(S.activation(T.sg[:, NS[1] * j:NS[1] * j + 16 * m], T.pr[:, 0:16 * m], F.Sign, scale=-1.0, bias=T.sc[:, 16 * m + 15:16 * m + 16])))
+                if j > 0:
+                    m = ROWS[i][j - 1]
+                    need("s", sg[j - 1])
+                    own_q[i] = s(S.activation(T.ft[:, f0 + j - 1:f0 + 64 * m:4], T.sg[:, NS[1] * (j - 1):NS[1] * (j - 1) + 16 * m], F.Relu, accum_out=T.rs[:, m:m + 1]))
+        need("v", d_sc, d_pr, *z)
+        quant, waiting, last_s = {}, None, None
+        todo = [i for i in range(8) if i not in MINE]
+        for i in todo:
+            f0 = 4 * CO[i]
+            for j, m in enumerate(ROWS[i]):
+                if m < 0:
+                    d = d_dg = v(V.tensor_tensor(T.ft[:, f0 + j:f0 + 4 * C:4], T.pp[:], T.sc[:], A.is_le))
+                else:
+                    d = v(V.tensor_scalar(T.ft[:, f0 + j:f0 + 64 * m:4], T.pp[:, 0:16 * m], T.sc[:, 16 * m + 15:16 * m + 16], None, A.is_lt))
+                    jo = 512 * (len(jd) % 4)
+                    need("s", d, *jd[-4:-3])
+                    last_s = s(S.activation(T.junk[:, jo:jo + 16 * m], T.ft[:, f0 + j:f0 + 64 * m:4], F.Copy, accum_out=T.rs[:, m:m + 1]))
+                    jd.append(last_s)
+                if waiting is not None and j == 1:
+                    quant[waiting[0]] = quantise_flags(*waiting)
+                    waiting = None
+                if i == todo[1] and j == 2:
+                    if t == 0:
+                        need("v", k_b1)
+                        c_bq = v(V.quantize_mx(T.bq[:], T.bs[:], T.bt[:]))
+                    need("v", d_dg, c_hold)
+                    d_cum = v(V.tensor_tensor_scan(T.cum[:], T.hold[:], T.ft[:, 0:4 * C:4], 0.0, A.mult, A.add))
+                if i == todo[3] and j == 2:
+                    need("v", d_cum, c_ac0)
+                    d_a1 = v(V.tensor_tensor(T.a1[:], T.ac0[:], T.cum[:, 15:512:16], A.subtract))
+                    for k in MINE: quant[k] = quantise_flags(k, own_q[k])
+            waiting = (i, d)
+        quant[waiting[0]] = quantise_flags(*waiting)
+        order = sorted(quant, key=lambda i: quant[i][1])
+        for i in order:
+            need("p", quant[i], c_bq)
+            d_pc = p(P.matmul_mx(T.pc[:, 0:NS[i]], T.bq[:], T.bs[:], T.fq[:, CO[i]:CO[i] + NS[i]], T.fs[:, CO[i]:CO[i] + NS[i]], i == order[0], i == order[-1]))
+        need("v", d_a1, last_s)
+        d_a2 = v(V.tensor_tensor(T.a2[:], T.a1[:], T.rs[:], A.subtract))
+        need("v", d_a2, c_sc)
+        d_a2s = v(V.tensor_scalar(T.a2s[:], T.a2[:], T.scol[:], None, A.mult))
+        need("v", d_pc, c_hk)
+        d_e1 = v(V.tensor_tensor_scan(T.e1[:], T.hk[:], T.pc[:], 0.0, A.mult, A.max))
+        need("v", d_e1, d_a2s)
+        d_a3 = v(V.tensor_tensor(T.a3[:], T.e1[:, 15:512:16], T.a2s[:], A.add))
+        need("v", d_a3, c_isc)
+        d_il = v(V.tensor_scalar(T.il[:], T.a3[:], T.isc[:], None, A.mult))
+        need("v", d_il, k_io)
+        d_inv = v(V.tensor_copy(T.inv[:, 0:512].indirect(T.il[:, 0:32]), T.iot[:]))
+        need("v", d_inv)
+        d_e2 = v(V.tensor_tensor_scan(T.e2[:], T.hk[:], T.inv[:], 0.0, A.mult, A.max))
+        need("v", d_e2, c_isc4)
+        dl = {}
+        for i in (2, 0, 3, 1):
+            dl[i] = v(V.tensor_scalar(T["l%d" % i][:], T.e2[:, 15:512:16], T.isc4[:], float(i - 4), A.mult, A.add))
+        for h in range(2):
+            o = {}
+            for i in (2, 3):
+                need("s", dl[i])
+                o[i] = s(S.activation(T.st[:, 1024 * h + i:1024 * h + 1024:4], X[:, 0:2048].indirect(T["l%d" % i][:, 16 * h:16 * h + 16]), F.Copy))
+            for i in (0, 1):
+                need("v", dl[i])
+                o[i] = v(V.tensor_copy(T.st[:, 1024 * h + i:1024 * h + 1024:4], X[:, 0:2048].indirect(T["l%d" % i][:, 16 * h:16 * h + 16])))
+            need("v", *o.values())
+            d_q = v(V.quantize_mx(SQ[:, 256 * h:256 * h + 256], SS[:, 256 * h:256 * h + 256], T.st[:, 1024 * h:1024 * h + 1024]))
+            need("g", d_q)
+            blocks = [4 * h + k for k in range(4)]
+            for kind in range(2):
+                tr, k = [], 0
+                for b in blocks:
+                    r = ow[b]
+                    if r == rank: continue
+                    if r in mate: es = ne
+                    else:
+                        es = pairs[TURN[h][kind][k]]
+                        k += 1
+                    if kind == 0: sv, dv = SQ[:, BL * b:BL * b + BL].bitcast(dt.uint8), LC[:, BL * rank:BL * rank + BL].bitcast(dt.uint8)
+                    else: sv, dv = SS[:, BL * b:BL * b + BL], LS[:, BL * rank:BL * rank + BL]
+                    tr.append(put(sv, [r], dv, "sa%d_%d" % (t, rank), es))
+                g.remote_dma_fused(tr, local_sem=sem.lsem)
+            if own in blocks:
+                need("y", d_q)
+                Y.dma_start(LC[:, BL * rank:BL * rank + BL].bitcast(dt.uint8), SQ[:, BL * own:BL * own + BL].bitcast(dt.uint8)).then_inc(sem["cs%d" % t], 16)
+                Y.dma_start(LS[:, BL * rank:BL * rank + BL], SS[:, BL * own:BL * own + BL]).then_inc(sem["cs%d" % t], 16)
+        if t == 0:
+            need("v", k_eb)
+            c_eq = v(V.quantize_mx(T.eq[:], T.es[:], T.eb[:]))
+            c_mt = v(V.memset(T.mt[:], 0.0))
+            c_ht = v(V.memset(T.ht[:], 0.0))
+            need("v", c_mt)
+            for w in range(R): pad = v(V.quantize_mx(T["lc%d" % w][:, 512:640], T["ls%d" % w][:, 512:640], T.mt[:]))
+        d_sh = v(V.tensor_scalar(T.sh[:], T.st[:], 0.125, None, A.mult))
+        if last:
+            d_ol = v(V.tensor_scalar(T.olt[:], T.inv[:], -1.0, None, A.add))
+            need("v", ("lv", 16))
+            c_vq = v(V.quantize_mx(T.vq[:], T.vsc[:], T.vt[:]))
+        need("p", d_q, c_eq)
+        arrived = lambda r: ("cs%d" % t, 32) if r == rank else ("sa%d_%d" % (t, r), 2 * len(ne) if r in mate else 4)
+        E = lambda b: (T.eq[:, 128 * b:128 * b + 128], T.es[:, 128 * b:128 * b + 128])
+        part = {(0, b): (T.pa, 512 * b) for b in (1, 2, 3)}
+        part.update({(1, 1): (T.pp, 0), (1, 2): (T.pc, 0), (1, 3): (T.pe, 0)})
+
+        def in_bank(r):
+            if r == 7: need("p", pad)
+            return p(P.matmul_mx(T.pa[:, 0:128], *E(0), LC[:, BL * r:BL * r + 128], LS[:, BL * r:BL * r + 128], r == 0, r == 7))
+
+        d_u = {}
+        for h in range(2):
+            for r in range(4): need("p", arrived(4 * h + r))
+            for b in (1, 2, 3):
+                q, c = part[h, b]
+                d_u[h, b] = p(P.matmul_mx(q[:, c:c + 256], *E(b), LC[:, 256 * h:256 * h + 256], LS[:, 256 * h:256 * h + 256], True, True))
+            for r in ((0, 1, 2) if h == 0 else (3, 4, 5, 6, 7)): d_m0 = in_bank(r)
+        acc = {}
+        for b in (1, 2, 3):
+            need("s", d_u[0, b])
+            acc[b] = s(S.activation(T.acb[:, 64 * (b - 1):64 * b], T.pa[:, 512 * b:512 * b + 64], F.Copy))
+        need("v", c_mt)
+        for r in range(1, 8):
+            for b in (1, 2, 3):
+                q, c = part[r // 4, b]
+                c += 64 * (r % 4)
+                need("v", d_u[r // 4, b], acc[b])
+                out = T.acb[:, 64 * (b - 1):64 * b] if r < 7 else T.mt[:, b:256:4]
+                acc[b] = v(V.tensor_tensor(out, q[:, c:c + 64], T.acb[:, 64 * (b - 1):64 * b], A.add))
+        need("s", d_m0, c_mt)
+        d = s(S.activation(T.mt[:, 0:256:4], T.pa[:, 0:64], F.Copy))
+        need("v", d, *acc.values())
+        d_mq = v(V.quantize_mx(T.mq[:], T.ms[:], T.mt[:]))
+        need("p", d_mq, ("lw", 16), ("lws", 16))
+        d_h = [p(P.matmul_mx(T.pa[:, 512 * b:512 * b + 128], T.wq[:, 128 * b:128 * b + 128], T.wsc[:, 128 * b:128 * b + 128], T.mq[:], T.ms[:], True, True)) for b in range(4)]
+        o = []
+        for b in range(4):
+            need("s" if b % 2 == 0 else "v", d_h[b], c_ht)
+            if b % 2 == 0: o.append(s(S.activation(T.ht[:, b:256:4], T.pa[:, 512 * b:512 * b + 64], F.Relu, scale=0.0625)))
+            else: o.append(v(V.tensor_scalar(T.ht[:, b:256:4], T.pa[:, 512 * b:512 * b + 64], 0.0, 0.0625, A.max, A.mult)))
+        need("v", *o)
+        d_hq = v(V.quantize_mx(HQ[:], HS[:], T.ht[:]))
+        need("g", d_hq)
+        for kind in range(2):
+            if kind == 0: sv, dv = HQ[:, 0:BL].bitcast(dt.uint8), HL[:, BL * own:BL * own + BL].bitcast(dt.uint8)
+            else: sv, dv = HS[:, 0:BL], HP[:, BL * own:BL * own + BL]
+            g.remote_dma_fused([put(sv, far, dv, "ha%d" % t, fe), put(sv, mate, dv, "ha%d" % t, ne)], local_sem=sem.lsem)
+        need("y", d_hq)
+        Y.dma_start(HL[:, BL * own:BL * own + BL].bitcast(dt.uint8), HQ[:, 0:BL].bitcast(dt.uint8)).then_inc(sem["ch%d" % t], 16)
+        Y.dma_start(HP[:, BL * own:BL * own + BL], HS[:, 0:BL]).then_inc(sem["ch%d" % t], 16)
+        if last:
+            need("y", d_ol)
+            Y.dma_start(T.ol[:, :], T.olt[0:128:16, :]).then_inc(sem.so, 16)
+        need("p", d_hq, ("ch%d" % t, 32), ("ha%d" % t, 2 * (len(far) * len(fe) + len(ne))))
+        d_b = [p(P.matmul_mx(T.pa[:, 512 * b:512 * b + 512], *E(b), HL[:], HP[:], True, True)) for b in range(4)]
+        o = []
+        for b in range(4):
+            need("v", d_b[b], d_sh)
+            w = T.sn[:, 512 * b:512 * b + 512]
+            d = v(V.tensor_tensor(w, T.pa[:, 512 * b:512 * b + 512], T.sh[:, b:2048:4], A.add))
+            if b < 3:
+                need("s", d)
+                o.append(s(S.activation(XN[:, b:2048:4], w.indirect(T.il[:, 0:32]), F.Copy, scale=4.0)))
+            else:
+                need("v", d)
+                o.append(v(V.tensor_scalar(XN[:, b:2048:4], w.indirect(T.il[:, 0:32]), 4.0, None, A.mult)))
+        need("v", *o)
+        xq = v(V.quantize_mx(T["xq%d" % (t + 1)][:], T["xs%d" % (t + 1)][:], XN[:]))
+
+    XQ, XS = T["xq%d" % R], T["xs%d" % R]
+    need("y", xq)
+    Y.dma_start(T.oc[:, :], XQ[:].bitcast(dt.uint8)).then_inc(sem.so, 16)
+    for k in range(4): Y.dma_start(T.osc[4 * k:4 * k + 4, :], XS[32 * k:32 * k + 4, :]).then_inc(sem.so, 16)
+    need("p", xq, c_vq)
+    d_y = [p(P.matmul_mx(b[:, 0:256], T.vq[:], T.vsc[:], XQ[:, 256 * k:256 * k + 256], XS[:, 256 * k:256 * k + 256], True, True)) for k, b in enumerate((T.pp, T.pc))]
+    need("v", d_y[0])
+    y0 = v(V.tensor_copy(T.yt[:, 0:256], T.pp[:, 0:256]))
+    need("s", d_y[1])
+    y1 = s(S.activation(T.yt[:, 256:512], T.pc[:, 0:256], F.Copy))
+    need("y", y0)
+    Y.dma_start(T.y[:, 0:256], T.yt[:, 0:256]).then_inc(sem.so, 16)
+    need("s", y1)
+    S.dma_start(T.y[:, 256:512], T.yt[:, 256:512]).then_inc(sem.sy, 16)
+    need("s", ("sy", 16))
+    need("y", *[(k, n) for k, n in cnt.items()], ("so", 16 * 7))
+    need("g", ("lsem", local[0]))

@@ -9,8 +9,10 @@ NS = [512, 448, 384, 320, 256, 192, 128, 128]
 CO = [sum(NS[:s]) for s in range(8)]
 FC = sum(NS)
 ROWS = [[-1, 31, 30, 29]] + [[32 - 4 * s - t for t in range(4)] for s in range(1, 8)]
-MINE = [1]
+FOLD = {2: 128, 3: 160, 4: 128, 5: 192, 6: 128, 7: 128}
 BIG = 2.0 ** 94
+PK = 1024.0
+WHOLE = 1.5 * 2.0 ** 23
 
 E4, U8, BF, F32, I32, U16 = "float8_e4m3fn_x4", "uint8", "bfloat16", "float32", "int32", "uint16"
 SCRATCH = {}
@@ -26,25 +28,32 @@ def _mx(n, *pairs):
         _sb(n, U8, b)
 
 
-_sb(2048, BF, "x0", "x1", "x2", "st", "sh", "sn", "eb", "junk")
-_sb(512, BF, "ut", "vt", "bt", "bt2", "eighth", "mt", "ht", "c0", "bm", "maskb", "rst", "hold", "hk0", "hk")
-_sb(4 * NS[1], BF, "sg")
+_sb(2048, BF, "x0", "x1", "x2", "st", "sh", "sn", "eb")
+_sb(12 * 192, F32, "junk")
+_sb(512, BF, "ut", "vt", "bt", "bt2", "eighth", "mt", "ht", "c0", "bm", "maskb", "rst", "hold", "hk0", "hk", "cum")
+_sb(1024, BF, "fw")
+_sb(128, BF, "dj")
+_sb(7 * 512, BF, "sg")
 _sb(4 * FC, BF, "ft")
-_sb(512, F32, "iot", "pr", "pm", "sc", "cum", "e1", "e2", "inv", "olt", "yt")
+_sb(512, F32, "iot", "pr", "pm", "sc", "e1", "e2", "inv", "olt", "yt")
 _sb(192, F32, "acb")
-_sb(32, F32, "m0", "ac0", "rs", "a1", "a2", "a2s", "a3")
-_sb(1, F32, "pi", "pi1", "p15", "scol", "isc", "isc4")
+_sb(32, F32, "m0", "ac0", "rs", "cr", "a1", "a2", "a2b", "a2s")
+_sb(12, F32, "hw")
+_sb(1, F32, "pi", "pi1", "p15", "isc", "isc4")
 _sb(1, I32, "p0", "p1")
 _sb(8, I32, "uo0")
 _sb(8, U16, "uoff")
+_sb(32, F32, "a3")
 _sb(32, U16, "il", "l0", "l1", "l2", "l3")
 _mx(128, ("uq", "us"), ("ur", "urs"), ("vq", "vsc"), ("bq", "bs"), ("mq", "ms"), ("hq0", "hs0"), ("hq1", "hs1"))
+_mx(256, ("fwq", "fws"))
 _mx(512, ("wq", "wsc"), ("eq", "es"), ("xq0", "xs0"), ("xq1", "xs1"), ("xq2", "xs2"), ("sq0", "ss0"), ("sq1", "ss1"), ("hl0", "hp0"), ("hl1", "hp1"))
 _mx(640, ("lc0", "ls0"), ("lc1", "ls1"))
 _mx(FC, ("fq", "fs"))
-SCRATCH.update({"pp": ("psum", [128, 512], F32), "pc": ("psum", [128, 512], F32), "pe": ("psum", [128, 512], F32), "pa": ("psum", [128, 2048], F32)})
+SCRATCH.update({"pp": ("psum", [128, 512], F32), "pc": ("psum", [128, 512], F32), "pe": ("psum", [128, 512], F32), "pf": ("psum", [128, 512], F32),
+                "pa": ("psum", [128, 2048], F32)})
 SEMAPHORES = ["vs", "ss", "ps", "gs", "lx", "lu", "lv", "lw", "lws", "lsem", "so", "sy"]
-SEMAPHORES += ["sa%d_%d" % (t, r) for t in range(R) for r in range(8)] + ["%s%d" % (k, t) for t in range(R) for k in ("ha", "cs", "ch")]
+SEMAPHORES += ["sa%d_%d" % (t, r) for t in range(R) for r in range(8)] + ["%s%d" % (k, t) for t in range(R) for k in ("ha", "hb", "cs", "ch")]
 
 
 def owners(T, topo):
@@ -94,6 +103,7 @@ def rank_program(g, core, T, topo):
     k_p = gg(g.iota(T.p0[:], [[0, 1]], 0, 1))
     k_uo = gg(g.iota(T.uo0[:], [[16, 8]], 0, 0))
     k_c = gg(g.iota(T.c0[:], [[0, 32], [1, 16]], 0, 0, **small))
+    k_dj = gg(g.iota(T.dj[:], [[1, 128]], 0, -1, **small))
     k_m = gg(g.iota(T.m0[:], [[16, 32]], 15, 0, **small))
     c_8 = v(V.memset(T.eighth[:], 0.125))
     need("g", c_8)
@@ -107,6 +117,8 @@ def rank_program(g, core, T, topo):
     for i in range(8):
         w = 64 if i < 7 else 128
         z.append(v(V.memset(T.ft[:, 4 * (CO[i] + NS[i] - w):4 * (CO[i] + NS[i])], 0.0)))
+    c_fw = v(V.memset(T.fw[:], 0.0))
+    c_cr = v(V.memset(T.cr[:], 0.0))
     c_rs = v(V.memset(T.rs[:], 0.0))
     need("v", k_p)
     c_p = v(V.tensor_scalar(T.p1[:], T.p0[:], 15, None, A.bitwise_and))
@@ -130,15 +142,19 @@ def rank_program(g, core, T, topo):
     need("s", c_uq)
     c_urs = s(S.activation(T.urs[:, 0:128], T.us[:, 0:128].indirect(T.uoff[:, 0:8]), F.Copy))
     c_hk0 = v(V.tensor_scalar(T.hk0[:], T.c0[:], T.pi1[:], 1024.0, A.is_equal, A.mult))
+    need("v", k_dj, c_fw)
+    for j in range(4):
+        o = 512 * (j // 2) + j
+        c_f = v(V.tensor_scalar(T.fw[:, o:512 * (j // 2) + 512:4], T.dj[:], 0.0, PK if j % 2 else 1.0, A.is_equal, A.mult))
     need("v", ("lx", 16))
     xq = v(V.quantize_mx(T.xq0[:], T.xs0[:], T.x0[:]))
-    need("v", c_hk0)
-    c_hk = v(V.tensor_tensor(T.hk[:], T.hk0[:], T.bm[:], A.max))
-    c_sc = v(V.tensor_scalar(T.scol[:], T.p15[:], -127.875, 128.0, A.mult, A.add))
+    need("v", c_f)
+    c_fq = v(V.quantize_mx(T.fwq[:], T.fws[:], T.fw[:]))
     c_isc = v(V.tensor_scalar(T.isc[:], T.p15[:], 8.0 - 2.0 ** -7, 2.0 ** -7, A.mult, A.add))
     c_isc4 = v(V.tensor_scalar(T.isc4[:], T.p15[:], 4.0 - 2.0 ** -8, 2.0 ** -8, A.mult, A.add))
     need("v", k_m)
     c_ac0 = v(V.tensor_scalar(T.ac0[:], T.m0[:], T.pi[:], None, A.subtract))
+    c_hk = v(V.tensor_tensor(T.hk[:], T.hk0[:], T.bm[:], A.max))
 
     ow = owners(T, topo)
     own = ow.index(rank)
@@ -158,13 +174,8 @@ def rank_program(g, core, T, topo):
         return RemoteDMATransfer(dst_ids=ids, dma_engine_mask=sum(1 << e for e in es), remote_sem=sem[sm], srcs=[src], dsts=[dst] * len(rs))
 
     TURN = [([0, 1, 2], [3, 0, 1]), ([3, 2, 0], [1, 2, 3])]
+    BANK = [(T.pa, 0), (T.pa, 512), (T.pa, 1024), (T.pa, 1536), (T.pe, 0), (T.pf, 0)]
 
-    def quantise_flags(i, d):
-        need("v", d)
-        a, b = CO[i], CO[i] + NS[i]
-        return v(V.quantize_mx(T.fq[:, a:b], T.fs[:, a:b], T.ft[:, 4 * a:4 * b]))
-
-    jd = []
     for t in range(R):
         X, XN = T["x%d" % t], T["x%d" % (t + 1)]
         XQ, XS = T["xq%d" % t], T["xs%d" % t]
@@ -179,61 +190,105 @@ def rank_program(g, core, T, topo):
         d_pr = s(S.activation(T.pr[:], T.pp[:], F.Copy))
         need("v", d_pm, c_rst)
         d_sc = v(V.tensor_tensor_scan(T.sc[:], T.rst[:], T.pm[:], -BIG, A.min, A.max))
-        need("s", d_sc, c_rs, z[-1], d_pr)
-        own_q = {}
-        for i in MINE:
-            f0, sg = 4 * CO[i], []
-            for j in range(5):
-                if j < 4:
-                    m = ROWS[i][j]
-                    sg.append(s(S.activation(T.sg[:, NS[1] * j:NS[1] * j + 16 * m], T.pr[:, 0:16 * m], F.Sign, scale=-1.0, bias=T.sc[:, 16 * m + 15:16 * m + 16])))
-                if j > 0:
-                    m = ROWS[i][j - 1]
-                    need("s", sg[j - 1])
-                    own_q[i] = s(S.activation(T.ft[:, f0 + j - 1:f0 + 64 * m:4], T.sg[:, NS[1] * (j - 1):NS[1] * (j - 1) + 16 * m], F.Relu, accum_out=T.rs[:, m:m + 1]))
-        need("v", d_sc, d_pr, *z)
-        quant, waiting, last_s = {}, None, None
-        todo = [i for i in range(8) if i not in MINE]
-        for i in todo:
-            f0 = 4 * CO[i]
-            for j, m in enumerate(ROWS[i]):
-                if m < 0:
-                    d = d_dg = v(V.tensor_tensor(T.ft[:, f0 + j:f0 + 4 * C:4], T.pp[:], T.sc[:], A.is_le))
-                else:
-                    d = v(V.tensor_scalar(T.ft[:, f0 + j:f0 + 64 * m:4], T.pp[:, 0:16 * m], T.sc[:, 16 * m + 15:16 * m + 16], None, A.is_lt))
-                    jo = 512 * (len(jd) % 4)
-                    need("s", d, *jd[-4:-3])
-                    last_s = s(S.activation(T.junk[:, jo:jo + 16 * m], T.ft[:, f0 + j:f0 + 64 * m:4], F.Copy, accum_out=T.rs[:, m:m + 1]))
-                    jd.append(last_s)
-                if waiting is not None and j == 1:
-                    quant[waiting[0]] = quantise_flags(*waiting)
-                    waiting = None
-                if i == todo[1] and j == 2:
-                    if t == 0:
-                        need("v", k_b1)
-                        c_bq = v(V.quantize_mx(T.bq[:], T.bs[:], T.bt[:]))
-                    need("v", d_dg, c_hold)
-                    d_cum = v(V.tensor_tensor_scan(T.cum[:], T.hold[:], T.ft[:, 0:4 * C:4], 0.0, A.mult, A.add))
-                if i == todo[3] and j == 2:
-                    need("v", d_cum, c_ac0)
-                    d_a1 = v(V.tensor_tensor(T.a1[:], T.ac0[:], T.cum[:, 15:512:16], A.subtract))
-                    for k in MINE: quant[k] = quantise_flags(k, own_q[k])
-            waiting = (i, d)
-        quant[waiting[0]] = quantise_flags(*waiting)
-        order = sorted(quant, key=lambda i: quant[i][1])
-        for i in order:
+        sg, rl, fl, quant, fold, sums = {}, {}, {}, {}, {}, {}
+
+        def sign(m):
+            o = 512 * (31 - m)
+            sg[m] = s(S.activation(T.sg[:, o:o + 16 * m], T.pr[:, 0:16 * m], F.Sign, scale=-1.0, bias=T.sc[:, 16 * m + 15:16 * m + 16]))
+
+        def relu(m):
+            i, j, o = (0 if m > 28 else 1), (32 - m) % 4, 512 * (31 - m)
+            need("s", sg[m])
+            rl[m] = s(S.activation(T.ft[:, 4 * CO[i] + j:4 * CO[i] + 64 * m:4], T.sg[:, o:o + 16 * m], F.Relu, accum_out=T.rs[:, m:m + 1]))
+
+        def flags(i, js):
+            for j in js:
+                m = ROWS[i][j]
+                fl[i] = v(V.tensor_scalar(T.ft[:, 4 * CO[i] + j:4 * CO[i] + 64 * m:4], T.pp[:, 0:16 * m], T.sc[:, 16 * m + 15:16 * m + 16], None, A.is_lt))
+
+        def quantise(i, *d):
+            need("v", *d)
+            a, b = CO[i], CO[i] + NS[i]
+            quant[i] = v(V.quantize_mx(T.fq[:, a:b], T.fs[:, a:b], T.ft[:, 4 * a:4 * b]))
+
+        def folds(i):
+            need("p", quant[i], c_fq)
+            if i >= 5: need("p", sums[i - 3])
+            w = FOLD[i]
+            for k in range(2):
+                q, c = BANK[2 * ((i - 2) % 3) + k]
+                n = NS[i] // w
+                for e in range(n):
+                    a = CO[i] + w * e
+                    fold[i, k] = p(P.matmul_mx(q[:, c:c + w], T.fwq[:, 128 * k:128 * k + 128], T.fws[:, 128 * k:128 * k + 128], T.fq[:, a:a + w], T.fs[:, a:a + w], e == 0, e == n - 1))
+
+        def columns(i):
             need("p", quant[i], c_bq)
-            d_pc = p(P.matmul_mx(T.pc[:, 0:NS[i]], T.bq[:], T.bs[:], T.fq[:, CO[i]:CO[i] + NS[i]], T.fs[:, CO[i]:CO[i] + NS[i]], i == order[0], i == order[-1]))
-        need("v", d_a1, last_s)
-        d_a2 = v(V.tensor_tensor(T.a2[:], T.a1[:], T.rs[:], A.subtract))
-        need("v", d_a2, c_sc)
-        d_a2s = v(V.tensor_scalar(T.a2s[:], T.a2[:], T.scol[:], None, A.mult))
+            return p(P.matmul_mx(T.pc[:, 0:NS[i]], T.bq[:], T.bs[:], T.fq[:, CO[i]:CO[i] + NS[i]], T.fs[:, CO[i]:CO[i] + NS[i]], i == 0, i == 1))
+
+        def along(i):
+            for k in range(2):
+                q, c = BANK[2 * ((i - 2) % 3) + k]
+                m = ROWS[i][2 * k]
+                w = min(FOLD[i], 16 * m)
+                jo = 192 * (2 * (i - 2) + k)
+                need("s", fold[i, k])
+                sums[i] = s(S.activation(T.junk[:, jo:jo + w], q[:, c:c + w], F.Copy, accum_out=T.rs[:, m:m + 1]))
+
+        need("s", d_sc, c_rs, z[-1], d_pr)
+        need("v", d_sc, d_pr, *z)
+        sign(31); sign(30); relu(31); sign(29); relu(30); sign(28); relu(29)
+        flags(2, range(4))
+        d_dg = v(V.tensor_tensor(T.ft[:, 0:4 * C:4], T.pp[:], T.sc[:], A.is_le))
+        quantise(2, fl[2])
+        folds(2)
+        flags(3, range(4))
+        if t == 0:
+            need("v", k_b1)
+            c_bq = v(V.quantize_mx(T.bq[:], T.bs[:], T.bt[:]))
+        need("v", d_dg, c_hold)
+        d_cum = v(V.tensor_tensor_scan(T.cum[:], T.hold[:], T.ft[:, 0:4 * C:4], 0.0, A.mult, A.add))
+        quantise(3, fl[3])
+        folds(3)
+        relu(28); along(2); sign(27); sign(26); relu(27); along(3); sign(25); relu(26); relu(25)
+        quantise(0, d_dg, rl[29])
+        columns(0); columns(2); columns(3)
+        flags(4, range(4))
+        flags(5, [0])
+        quantise(4, fl[4])
+        folds(4); columns(4)
+        flags(5, [1, 2, 3])
+        flags(6, [0])
+        quantise(5, fl[5])
+        folds(5); columns(5)
+        along(4); along(5)
+        flags(6, [1, 2, 3])
+        flags(7, range(4))
+        quantise(6, fl[6])
+        quantise(7, fl[7])
+        quantise(1, rl[25])
+        folds(6); folds(7); columns(6); columns(7)
+        d_pc = columns(1)
+        along(6); along(7)
+        need("s", sums[7], c_cr)
+        d_hw = s(S.activation(T.hw[:], T.rs[:, 2:25:2], F.Copy, scale=1.0 / PK, bias=WHOLE))
+        need("s", d_hw)
+        d_odd = s(S.activation(T.rs[:, 1:24:2], T.hw[:], F.Copy, bias=-WHOLE))
+        d_cr = s(S.activation(T.cr[:, 2:25:2], T.hw[:], F.Copy, scale=PK, bias=-WHOLE * PK))
+        need("v", d_cum, c_ac0)
+        d_a1 = v(V.tensor_tensor(T.a1[:], T.ac0[:], T.cum[:, 15:512:16], A.subtract))
         need("v", d_pc, c_hk)
         d_e1 = v(V.tensor_tensor_scan(T.e1[:], T.hk[:], T.pc[:], 0.0, A.mult, A.max))
-        need("v", d_e1, d_a2s)
-        d_a3 = v(V.tensor_tensor(T.a3[:], T.e1[:, 15:512:16], T.a2s[:], A.add))
-        need("v", d_a3, c_isc)
-        d_il = v(V.tensor_scalar(T.il[:], T.a3[:], T.isc[:], None, A.mult))
+        need("v", d_a1, d_odd)
+        d_a2 = v(V.tensor_tensor(T.a2[:], T.a1[:], T.rs[:], A.subtract))
+        need("v", d_e1, c_isc)
+        d_a2s = v(V.tensor_scalar(T.a2s[:], T.e1[:, 15:512:16], T.isc[:], None, A.mult))
+        need("v", d_a2, d_cr)
+        d_a2 = v(V.tensor_tensor(T.a2b[:], T.a2[:], T.cr[:], A.add))
+        need("v", d_a2, d_a2s)
+        d_a3 = v(V.tensor_tensor(T.a3[:], T.a2b[:], T.a2s[:], A.add))
+        need("v", d_a3)
+        d_il = v(V.tensor_copy(T.il[:], T.a3[:]))
         need("v", d_il, k_io)
         d_inv = v(V.tensor_copy(T.inv[:, 0:512].indirect(T.il[:, 0:32]), T.iot[:]))
         need("v", d_inv)
@@ -326,29 +381,36 @@ def rank_program(g, core, T, topo):
         need("v", *o)
         d_hq = v(V.quantize_mx(HQ[:], HS[:], T.ht[:]))
         need("g", d_hq)
+        hsem = ["ha%d" % t, "hb%d" % t]
         for kind in range(2):
             if kind == 0: sv, dv = HQ[:, 0:BL].bitcast(dt.uint8), HL[:, BL * own:BL * own + BL].bitcast(dt.uint8)
             else: sv, dv = HS[:, 0:BL], HP[:, BL * own:BL * own + BL]
-            g.remote_dma_fused([put(sv, far, dv, "ha%d" % t, fe), put(sv, mate, dv, "ha%d" % t, ne)], local_sem=sem.lsem)
+            g.remote_dma_fused([put(sv, far, dv, hsem[own // 4], fe), put(sv, mate, dv, hsem[own // 4], ne)], local_sem=sem.lsem)
         need("y", d_hq)
         Y.dma_start(HL[:, BL * own:BL * own + BL].bitcast(dt.uint8), HQ[:, 0:BL].bitcast(dt.uint8)).then_inc(sem["ch%d" % t], 16)
         Y.dma_start(HP[:, BL * own:BL * own + BL], HS[:, 0:BL]).then_inc(sem["ch%d" % t], 16)
         if last:
             need("y", d_ol)
             Y.dma_start(T.ol[:, :], T.olt[0:128:16, :]).then_inc(sem.so, 16)
-        need("p", d_hq, ("ch%d" % t, 32), ("ha%d" % t, 2 * (len(far) * len(fe) + len(ne))))
-        d_b = [p(P.matmul_mx(T.pa[:, 512 * b:512 * b + 512], *E(b), HL[:], HP[:], True, True)) for b in range(4)]
+        need("p", d_hq)
+        add = {}
+        for h in range(2):
+            rs = [r for r in ow[4 * h:4 * h + 4] if r != rank]
+            need("p", (hsem[h], 2 * sum(len(ne) if r in mate else len(fe) for r in rs)))
+            if own // 4 == h: need("p", ("ch%d" % t, 32))
+            bank = [(T.pa, 512 * b) for b in range(4)] if h == 0 else [(T.pp, 0), (T.pc, 0), (T.pe, 0), (T.pf, 0)]
+            for b in (0, 1, 3, 2):
+                q, c = bank[b]
+                d = p(P.matmul_mx(q[:, c:c + 256], *E(b), HL[:, 256 * h:256 * h + 256], HP[:, 256 * h:256 * h + 256], True, True))
+                need("v", d, d_sh)
+                a = 512 * b + 256 * h
+                add[b] = v(V.tensor_tensor(T.sn[:, a:a + 256], q[:, c:c + 256], T.sh[:, 1024 * h + b:1024 * h + 1024:4], A.add))
         o = []
-        for b in range(4):
-            need("v", d_b[b], d_sh)
-            w = T.sn[:, 512 * b:512 * b + 512]
-            d = v(V.tensor_tensor(w, T.pa[:, 512 * b:512 * b + 512], T.sh[:, b:2048:4], A.add))
-            if b < 3:
-                need("s", d)
-                o.append(s(S.activation(XN[:, b:2048:4], w.indirect(T.il[:, 0:32]), F.Copy, scale=4.0)))
-            else:
-                need("v", d)
-                o.append(v(V.tensor_scalar(XN[:, b:2048:4], w.indirect(T.il[:, 0:32]), 4.0, None, A.mult)))
+        for q, b, a, e in (("s", 0, 0, 2), ("s", 1, 0, 2), ("v", 3, 0, 2), ("s", 2, 0, 1), ("v", 2, 1, 2)):
+            need(q, add[b])
+            w, out = T.sn[:, 512 * b:512 * b + 512].indirect(T.il[:, 16 * a:16 * e]), XN[:, 1024 * a + b:1024 * e:4]
+            if q == "s": o.append(s(S.activation(out, w, F.Copy, scale=4.0)))
+            else: o.append(v(V.tensor_scalar(out, w, 4.0, None, A.mult)))
         need("v", *o)
         xq = v(V.quantize_mx(T["xq%d" % (t + 1)][:], T["xs%d" % (t + 1)][:], XN[:]))
 
@@ -362,10 +424,9 @@ def rank_program(g, core, T, topo):
     y0 = v(V.tensor_copy(T.yt[:, 0:256], T.pp[:, 0:256]))
     need("s", d_y[1])
     y1 = s(S.activation(T.yt[:, 256:512], T.pc[:, 0:256], F.Copy))
-    need("y", y0)
-    Y.dma_start(T.y[:, 0:256], T.yt[:, 0:256]).then_inc(sem.so, 16)
-    need("s", y1)
-    S.dma_start(T.y[:, 256:512], T.yt[:, 256:512]).then_inc(sem.sy, 16)
+    need("g", y0)
+    g.wait_ge(sem.lsem, local[0])
+    need("s", y0, y1)
+    S.dma_start(T.y[:, :], T.yt[:, :]).then_inc(sem.sy, 16)
     need("s", ("sy", 16))
-    need("y", *[(k, n) for k, n in cnt.items()], ("so", 16 * 7))
-    need("g", ("lsem", local[0]))
+    need("y", *[(k, n) for k, n in cnt.items()], ("so", 16 * 6))

@@ -8,11 +8,31 @@ BL = 64
 NS = [512, 448, 384, 320, 256, 192, 128, 128]
 CO = [sum(NS[:s]) for s in range(8)]
 FC = sum(NS)
-ROWS = [[-1, 31, 30, 29]] + [[32 - 4 * s - t for t in range(4)] for s in range(1, 8)]
-FOLD = {2: 128, 3: 160, 4: 128, 5: 192, 6: 128, 7: 128}
+FOLD = {1: 224, 2: 128, 3: 160, 4: 128, 5: 192, 6: 128}
 BIG = 2.0 ** 94
 PK = 1024.0
 WHOLE = 1.5 * 2.0 ** 23
+KP, SIDE = 4, (2, 3)
+
+PLAN = [
+    {"v": "_c8 _z1 _z2 _p1 _rs0 _z0 _z7 _pi _z4 _z6 _z5 _hk0 _uoff _z3 _rst _uq _p15 _rep _bn _hk2 _ur qA _ac0 _cr0 qB _hk1 _isc pmA pmD fq scD scA f19 f4 f17 f22 f23 f18 "
+          "f21 f3 f20 f24 f15 f1 q2 bq f16 dg q3 f9 q0 f13 f14 f11 f12 q4 f5 q5 f2 f7 f8 f6 q7 cum q6 q1 a1 e1 a2 a2b a3 il inv e20 lo0 e21 t0_0_16 lo1 t3_0_16 t2_16_24 "
+          "sq0 t1_16_32 sq1",
+     "s": "_fw01 _fw00 _off _dja _maskb _urs _hold _fw1 _fw0 _fw2 _fw3 hk s29 s28 s30 s27 r29 s31 s26 s10 r31 r30 s25 r10 d4 r26 a22 a24 r28 r25 a20 r27 a14 a18 a12 a10 "
+          "a16 a6 a8 d2 hw d1 d3 t2_0_16 t1_0_16 t3_16_32 t2_24_32 t0_16_32",
+     "p": "sA sB sZ sY sX o24 o22 o20 o18 c0 c3 c2 o14 c5 o12 o10 c4 c7 o16 o6 c6 o8 c1",
+     "pairs": (6, 24)},
+    {"v": "w0 w1 w2 w3 x1_6_16 x3_0_10 qA x2_22_28 pmA x2_16_22 scA qB f14 f10 pmD scD f9 f16 f22 f23 f21 q4 dg f24 q5 f17 q2 f5 f18 f20 q0 f19 f25 q3 f6 f8 f26 q6 f2 f4 "
+          "q1 f3 f1 cum q7 a1 e1 a2 a2b a3 il inv e20 lo0 e21 t0_0_16 lo1 t3_0_16 t2_16_24 sq0 t1_16_32 sq1",
+     "s": "x0_0_16 x1_0_6 x2_0_16 x3_10_16 x1_16_32 x2_28_32 x3_16_32 x0_16_32 s11 s12 s15 s13 r15 r12 r11 s31 r13 s29 s7 s30 r29 r30 r31 s27 a16 r7 a10 a14 a22 s28 r27 "
+          "r28 a24 a12 a18 a8 a6 a20 a26 d1 hw d2 d4 d3 t2_0_16 t1_0_16 t3_16_32 t2_24_32 t0_16_32",
+     "p": "sA sX sB sZ sY o16 o10 o22 o14 o24 o12 c0 c2 c4 c5 c3 o18 o20 o6 o8 c6 o26 c1 c7",
+     "pairs": (6, 26)},
+    {"v": "w0 w1 w2 w3 x2_0_16 x3_0_24 x2_24_32 q0 q1 y1",
+     "s": "x0_0_24 x1_0_24 x2_16_24 x1_24_32 x3_24_32 x0_24_32 y0 Y1",
+     "y": "C0 O2 C1 O3 O1 O0 Y0",
+     "cuts": [0, 24, 32]},
+]
 
 E4, U8, BF, F32, I32, U16 = "float8_e4m3fn_x4", "uint8", "bfloat16", "float32", "int32", "uint16"
 SCRATCH = {}
@@ -28,23 +48,23 @@ def _mx(n, *pairs):
         _sb(n, U8, b)
 
 
-_sb(2048, BF, "x0", "x1", "x2", "st", "sh", "sn", "eb")
-_sb(12 * 192, F32, "junk")
-_sb(512, BF, "ut", "vt", "bt", "bt2", "eighth", "mt", "ht", "c0", "bm", "maskb", "rst", "hold", "hk0", "hk", "cum")
+_sb(2048, BF, "x0", "x1", "x2", "xp0", "xp1", "st", "sh", "sn", "eb")
+_sb(16 * 224, F32, "junk")
+_sb(512, BF, "ut", "vt", "bt", "bt2", "bw", "eighth", "mt", "ht", "c0", "off", "maskb", "rst", "hold", "hk", "cum")
 _sb(1024, BF, "fw")
-_sb(128, BF, "dj")
-_sb(7 * 512, BF, "sg")
+_sb(128, BF, "dj", "dja")
+_sb(16, BF, "hk0", "hk1", "hk2", "bm")
+_sb(11 * 512, BF, "sg")
 _sb(4 * FC, BF, "ft")
-_sb(512, F32, "iot", "pr", "pm", "sc", "e1", "e2", "inv", "olt", "yt")
-_sb(192, F32, "acb")
-_sb(32, F32, "m0", "ac0", "rs", "cr", "a1", "a2", "a2b", "a2s")
-_sb(12, F32, "hw")
-_sb(1, F32, "pi", "pi1", "p15", "isc", "isc4")
+_sb(512, F32, "iot", "pm", "sc", "e1", "e2", "inv", "olt", "yt")
+_sb(256, F32, "acb")
+_sb(32, F32, "m0", "ac0", "rs", "cr", "a1", "a2", "a2b", "a3")
+_sb(16, F32, "hw")
+_sb(1, F32, "pi", "p15", "isc")
 _sb(1, I32, "p0", "p1")
 _sb(8, I32, "uo0")
 _sb(8, U16, "uoff")
-_sb(32, F32, "a3")
-_sb(32, U16, "il", "l0", "l1", "l2", "l3")
+_sb(32, U16, "il", "lo", "rep")
 _mx(128, ("uq", "us"), ("ur", "urs"), ("vq", "vsc"), ("bq", "bs"), ("mq", "ms"), ("hq0", "hs0"), ("hq1", "hs1"))
 _mx(256, ("fwq", "fws"))
 _mx(512, ("wq", "wsc"), ("eq", "es"), ("xq0", "xs0"), ("xq1", "xs1"), ("xq2", "xs2"), ("sq0", "ss0"), ("sq1", "ss1"), ("hl0", "hp0"), ("hl1", "hp1"))
@@ -52,7 +72,7 @@ _mx(640, ("lc0", "ls0"), ("lc1", "ls1"))
 _mx(FC, ("fq", "fs"))
 SCRATCH.update({"pp": ("psum", [128, 512], F32), "pc": ("psum", [128, 512], F32), "pe": ("psum", [128, 512], F32), "pf": ("psum", [128, 512], F32),
                 "pa": ("psum", [128, 2048], F32)})
-SEMAPHORES = ["vs", "ss", "ps", "gs", "lx", "lu", "lv", "lw", "lws", "lsem", "so", "sy"]
+SEMAPHORES = ["vs", "ss", "ps", "gs", "lxa", "lxb", "lu", "lv", "lw", "lws", "lsem", "so"]
 SEMAPHORES += ["sa%d_%d" % (t, r) for t in range(R) for r in range(8)] + ["%s%d" % (k, t) for t in range(R) for k in ("ha", "hb", "cs", "ch")]
 
 
@@ -66,6 +86,10 @@ def owners(T, topo):
     return first + second
 
 
+def slot(m):
+    return (32 - m) // 4, (32 - m) % 4
+
+
 def rank_program(g, core, T, topo):
     rank = T.rank_of(core)
     if rank is None: return
@@ -73,88 +97,75 @@ def rank_program(g, core, T, topo):
     V, S, P, Y = g.vector, g.scalar, g.tensor, g.sync
     Q = {"g": g, "v": V, "s": S, "p": P, "y": Y}
     SEM = {"v": "vs", "s": "ss", "p": "ps", "g": "gs"}
-    cnt = {"vs": 0, "ss": 0, "ps": 0, "gs": 0}
-    seen = {q: {} for q in Q}
+    calls = {q: [] for q in Q}
+    count = {q: 0 for q in SEM}
+    named = {}
 
-    def need(q, *deps):
-        for d in deps:
-            if seen[q].get(d[0], 0) < d[1]:
-                Q[q].wait_ge(sem[d[0]], d[1])
-                seen[q][d[0]] = d[1]
+    def op(q, name, fn, *deps):
+        count[q] += 1
+        named[name] = (SEM[q], count[q])
+        calls[q].append((fn, deps, True))
+        return name
 
-    def done(q, inst):
-        k = SEM[q]
-        inst.then_inc(sem[k], 1)
-        cnt[k] += 1
-        return (k, cnt[k])
+    def raw(q, fn, *deps):
+        calls[q].append((fn, deps, False))
 
-    def v(inst): return done("v", inst)
-    def s(inst): return done("s", inst)
-    def p(inst): return done("p", inst)
-    def gg(inst): return done("g", inst)
+    def v(*a): return op("v", *a)
+    def s(*a): return op("s", *a)
+    def p(*a): return op("p", *a)
+    def gg(*a): return op("g", *a)
 
-    Y.dma_start(T.x0[:], T.x[:, :]).then_inc(sem.lx, 16)
-    S.dma_start(T.ut[:], T.u[:, :]).then_inc(sem.lu, 16)
-    Y.dma_start(T.wq[:].bitcast(dt.uint8), T.wc[:, :]).then_inc(sem.lw, 16)
-    Y.dma_start(T.wsc[:], T.ws[:, :]).then_inc(sem.lws, 16)
-    Y.dma_start(T.vt[:], T.v[:, :]).then_inc(sem.lv, 16)
+    raw("s", lambda: S.dma_start(T.ut[:], T.u[:, :]).then_inc(sem.lu, 16))
+    raw("y", lambda: Y.dma_start(T.x0[:, 0:1024], T.x[:, 0:1024]).then_inc(sem.lxa, 16))
+    raw("y", lambda: Y.dma_start(T.x0[:, 1024:2048], T.x[:, 1024:2048]).then_inc(sem.lxb, 16))
+    raw("y", lambda: Y.dma_start(T.wq[:].bitcast(dt.uint8), T.wc[:, :]).then_inc(sem.lw, 16), ("lxa", 16), ("lxb", 16))
+    raw("y", lambda: Y.dma_start(T.wsc[:], T.ws[:, :]).then_inc(sem.lws, 16))
+    raw("y", lambda: Y.dma_start(T.vt[:], T.v[:, :]).then_inc(sem.lv, 16))
 
     small = {"allow_small_or_imprecise_dtypes": True}
-    k_p = gg(g.iota(T.p0[:], [[0, 1]], 0, 1))
-    k_uo = gg(g.iota(T.uo0[:], [[16, 8]], 0, 0))
-    k_c = gg(g.iota(T.c0[:], [[0, 32], [1, 16]], 0, 0, **small))
-    k_dj = gg(g.iota(T.dj[:], [[1, 128]], 0, -1, **small))
-    k_m = gg(g.iota(T.m0[:], [[16, 32]], 15, 0, **small))
-    c_8 = v(V.memset(T.eighth[:], 0.125))
-    need("g", c_8)
-    k_b0 = gg(g.affine_select(T.bt2[:], T.eighth[:], [[-16, 8], [0, 64]], A.is_ge, 0.0, 0, 1))
-    need("g", k_b0)
-    k_b1 = gg(g.affine_select(T.bt[:], T.bt2[:], [[16, 8], [0, 64]], A.is_ge, 0.0, 15, -1))
-    k_io = gg(g.iota(T.iot[:], [[1, 512]], 1, 0, **small))
-    for b in range(4):
-        k_eb = gg(g.affine_select(T.eb[:, 512 * b:512 * b + 512], T.eighth[:], [[-1, 512]], A.is_equal, 0.0, b, 4))
-    z = []
+    gg("p0", lambda: g.iota(T.p0[:], [[0, 1]], 0, 1))
+    gg("c0", lambda: g.iota(T.c0[:], [[0, 32], [1, 16]], 0, 0, **small))
+    gg("uo0", lambda: g.iota(T.uo0[:], [[16, 8]], 0, 0))
+    gg("dj", lambda: g.iota(T.dj[:], [[1, 128]], 0, -1, **small))
+    gg("m0", lambda: g.iota(T.m0[:], [[16, 32]], 15, 0, **small))
+    gg("one", lambda: g.iota(T.bt2[:], [[0, 512]], 1, 0, **small))
+    gg("bw", lambda: g.affine_select(T.bw[:], T.bt2[:], [[0, 8], [1, 16], [0, 4]], A.is_equal, 2.0 ** -10, -15, 0), "one")
+    gg("b0", lambda: g.affine_select(T.bt2[:], T.bw[:], [[-16, 8], [0, 64]], A.is_ge, 0.0, 0, 1), "bw")
+    gg("b1", lambda: g.affine_select(T.bt[:], T.bt2[:], [[16, 8], [0, 64]], A.is_ge, 0.0, 15, -1), "b0")
+    gg("iot", lambda: g.iota(T.iot[:], [[1, 512]], 1, 0, **small))
+    K = {}
+
+    def const(name, fn, *deps): K[name] = (fn, deps)
+
+    const("c8", lambda: V.memset(T.eighth[:], 0.125))
     for i in range(8):
-        w = 64 if i < 7 else 128
-        z.append(v(V.memset(T.ft[:, 4 * (CO[i] + NS[i] - w):4 * (CO[i] + NS[i])], 0.0)))
-    c_fw = v(V.memset(T.fw[:], 0.0))
-    c_cr = v(V.memset(T.cr[:], 0.0))
-    c_rs = v(V.memset(T.rs[:], 0.0))
-    need("v", k_p)
-    c_p = v(V.tensor_scalar(T.p1[:], T.p0[:], 15, None, A.bitwise_and))
-    need("v", k_uo)
-    c_uoff = v(V.tensor_copy(T.uoff[:], T.uo0[:]))
-    need("v", c_p)
-    c_pi = v(V.tensor_copy(T.pi[:], T.p1[:]))
-    c_pi1 = v(V.tensor_scalar(T.pi1[:], T.p1[:], 1.0, None, A.add))
-    c_p15 = v(V.tensor_scalar(T.p15[:], T.p1[:], 15.0, None, A.is_equal))
-    need("v", k_c, c_pi)
-    c_bm = v(V.tensor_scalar(T.bm[:], T.c0[:], T.pi[:], None, A.not_equal))
-    need("s", c_bm)
-    c_mask = s(S.activation(T.maskb[:], T.bm[:], F.Copy, scale=-2.0 * BIG, bias=BIG))
-    c_hold = v(V.tensor_scalar(T.hold[:], T.c0[:], 1.0, None, A.min))
-    need("s", c_hold)
-    c_rst = s(S.activation(T.rst[:], T.hold[:], F.Copy, scale=2.0 * BIG, bias=-BIG))
-    need("v", ("lu", 16))
-    c_uq = v(V.quantize_mx(T.uq[:], T.us[:], T.ut[:]))
-    need("v", c_uq, c_uoff)
-    c_ur = v(V.tensor_copy(T.ur[:, 0:128].bitcast(dt.uint32), T.uq[:, 0:128].bitcast(dt.uint32).indirect(T.uoff[:, 0:8])))
-    need("s", c_uq)
-    c_urs = s(S.activation(T.urs[:, 0:128], T.us[:, 0:128].indirect(T.uoff[:, 0:8]), F.Copy))
-    c_hk0 = v(V.tensor_scalar(T.hk0[:], T.c0[:], T.pi1[:], 1024.0, A.is_equal, A.mult))
-    need("v", k_dj, c_fw)
+        w = 48 if i < 7 else 112
+        const("z%d" % i, lambda i=i, w=w: V.memset(T.ft[:, 4 * (CO[i] + NS[i] - w):4 * (CO[i] + NS[i])], 0.0))
+    const("cr0", lambda: V.memset(T.cr[:], 0.0))
+    const("rs0", lambda: V.memset(T.rs[:], 0.0))
+    const("rst", lambda: V.tensor_scalar(T.rst[:], T.c0[:], -0.5, 2.0 * BIG, A.add, A.mult), "c0")
+    const("p1", lambda: V.tensor_scalar(T.p1[:], T.p0[:], 15, None, A.bitwise_and), "p0")
+    const("uoff", lambda: V.tensor_copy(T.uoff[:], T.uo0[:]), "uo0")
+    const("pi", lambda: V.tensor_scalar(T.pi[:], T.p1[:], -1.0, None, A.mult), "p1")
+    const("uq", lambda: V.quantize_mx(T.uq[:], T.us[:], T.ut[:]), ("lu", 16))
+    const("ur", lambda: V.tensor_copy(T.ur[:, 0:128].bitcast(dt.uint32), T.uq[:, 0:128].bitcast(dt.uint32).indirect(T.uoff[:, 0:8])), "uq", "uoff")
+    const("hk0", lambda: V.tensor_scalar(T.hk0[:], T.c0[:, 0:16], T.pi[:], 1.0, A.add, A.is_equal), "pi", "c0")
+    const("hk2", lambda: V.tensor_scalar(T.hk2[:], T.hk0[:], 1023.0, 1.0, A.mult, A.add), "hk0")
+    const("hk1", lambda: V.tensor_tensor(T.hk1[:], T.hk2[:], T.bm[:, 0:16], A.mult), "hk2", "bn")
+    const("bn", lambda: V.tensor_scalar(T.bm[:, 0:16], T.c0[:, 0:16], T.pi[:], 0.0, A.add, A.not_equal), "pi", "c0")
+    const("rep", lambda: V.tensor_scalar(T.rep[:], T.m0[:], 0.0, T.pi[:], A.mult, A.subtract), "m0", "pi")
+    const("ac0", lambda: V.tensor_scalar(T.ac0[:], T.m0[:], T.pi[:], None, A.add), "m0", "pi")
+    const("p15", lambda: V.tensor_scalar(T.p15[:], T.p1[:], 15.0, 1.0 - 2.0 ** -10, A.is_equal, A.mult), "p1")
+    const("isc", lambda: V.tensor_scalar(T.isc[:], T.p15[:], 2.0 ** -10, None, A.add), "p15")
+    for k in range(2): const("fw0%d" % k, lambda k=k: S.activation(T.fw[:, 512 * k:512 * k + 512], T.eighth[:], F.Copy, scale=0.0), "c8")
+    const("off", lambda: S.activation(T.off[:], T.c0[:], F.Abs, bias=T.pi[:]), "c0", "pi")
+    const("maskb", lambda: S.activation(T.maskb[:], T.off[:], F.Copy, scale=-2.0 * BIG, bias=BIG), "off")
+    const("hold", lambda: S.activation(T.hold[:], T.c0[:], F.Sign), "c0")
+    const("urs", lambda: S.activation(T.urs[:, 0:128], T.us[:, 0:128].indirect(T.uoff[:, 0:8]), F.Copy), "uq", "uoff")
+    const("dja", lambda: S.activation(T.dja[:], T.dj[:], F.Abs), "dj")
     for j in range(4):
-        o = 512 * (j // 2) + j
-        c_f = v(V.tensor_scalar(T.fw[:, o:512 * (j // 2) + 512:4], T.dj[:], 0.0, PK if j % 2 else 1.0, A.is_equal, A.mult))
-    need("v", ("lx", 16))
-    xq = v(V.quantize_mx(T.xq0[:], T.xs0[:], T.x0[:]))
-    need("v", c_f)
-    c_fq = v(V.quantize_mx(T.fwq[:], T.fws[:], T.fw[:]))
-    c_isc = v(V.tensor_scalar(T.isc[:], T.p15[:], 8.0 - 2.0 ** -7, 2.0 ** -7, A.mult, A.add))
-    c_isc4 = v(V.tensor_scalar(T.isc4[:], T.p15[:], 4.0 - 2.0 ** -8, 2.0 ** -8, A.mult, A.add))
-    need("v", k_m)
-    c_ac0 = v(V.tensor_scalar(T.ac0[:], T.m0[:], T.pi[:], None, A.subtract))
-    c_hk = v(V.tensor_tensor(T.hk[:], T.hk0[:], T.bm[:], A.max))
+        w = PK if j % 2 else 1.0
+        const("fw%d" % j, lambda j=j, w=w: S.activation(T.fw[:, 512 * (j // 2) + j:512 * (j // 2) + 512:4], T.dja[:], F.Relu, scale=-w, bias=w), "dja", "fw0%d" % (j // 2))
 
     ow = owners(T, topo)
     own = ow.index(rank)
@@ -162,7 +173,7 @@ def rank_program(g, core, T, topo):
     far = [r for r in range(len(T.cores)) if topo.chip(T.cores[r]) != topo.chip(core)]
     fe = topo.engines(core, T.cores[far[0]])
     pairs = [fe[2 * k:2 * k + 2] for k in range(4)]
-    ne = [e for e in topo.engines(core, T.cores[mate[0]]) if e not in fe][:4]
+    ne = [e for e in topo.engines(core, T.cores[mate[0]]) if e not in fe][:2]
     local = [0]
 
     def put(src, rs, dst, sm, es):
@@ -174,140 +185,149 @@ def rank_program(g, core, T, topo):
         return RemoteDMATransfer(dst_ids=ids, dma_engine_mask=sum(1 << e for e in es), remote_sem=sem[sm], srcs=[src], dsts=[dst] * len(rs))
 
     TURN = [([0, 1, 2], [3, 0, 1]), ([3, 2, 0], [1, 2, 3])]
-    BANK = [(T.pa, 0), (T.pa, 512), (T.pa, 1024), (T.pa, 1536), (T.pe, 0), (T.pf, 0)]
+    BANK = [(T.pa, 0), (T.pa, 512), (T.pa, 1024), (T.pa, 1536), (T.pe, 0)]
 
-    for t in range(R):
-        X, XN = T["x%d" % t], T["x%d" % (t + 1)]
+    def pick(q, k, name, out, window, lst, scale, *ready):
+        b, a, e = [int(z) for z in k[1:].split("_")]
+        o, w = out[:, 64 * a + b:64 * e:4], window[:, 512 * b:512 * b + 512].indirect(lst[:, a:e])
+        if q == "s": s(name, lambda: S.activation(o, w, F.Copy, scale=scale), *ready)
+        elif scale == 1.0: v(name, lambda: V.tensor_copy(o, w), *ready)
+        else: v(name, lambda: V.tensor_scalar(o, w, scale, None, A.mult), *ready)
+
+    def covering(plan, t, letter, a, e):
+        return ["%s@%d" % (k, t) for q in "vs" for k in plan[q].split() if k[0] == letter and int(k.split("_")[1]) < e and int(k.split("_")[2]) > a]
+
+    def head(q, k, t):
+        b = int(k[1])
+        if k[0] == "w":
+            c, a = [T.pp, T.pc, T.pe, T.pf][b], 512 * b + 256
+            v("%s@%d" % (k, t), lambda: V.tensor_tensor(T.sn[:, a:a + 256], c[:, 0:256], T.sh[:, 1024 + b:2048:4], A.add), "d1%d@%d" % (b, t - 1))
+        else: pick(q, k, "%s@%d" % (k, t), T["x%d" % t], T.sn, T.il, 4.0, "w%d@%d" % (b, t))
+
+    def one_round(t):
+        X, XP = T["x%d" % t], T["xp%d" % t]
         XQ, XS = T["xq%d" % t], T["xs%d" % t]
         SQ, SS, LC, LS = T["sq%d" % t], T["ss%d" % t], T["lc%d" % t], T["ls%d" % t]
         HQ, HS, HL, HP = T["hq%d" % t], T["hs%d" % t], T["hl%d" % t], T["hp%d" % t]
         last = t == R - 1
-        need("p", xq, c_ur, c_urs)
-        d_p = p(P.matmul_mx(T.pp[:], T.ur[:], T.urs[:], XQ[:], XS[:], True, True))
-        need("v", d_p, c_mask)
-        d_pm = v(V.tensor_tensor(T.pm[:], T.pp[:], T.maskb[:], A.min))
-        need("s", d_pm)
-        d_pr = s(S.activation(T.pr[:], T.pp[:], F.Copy))
-        need("v", d_pm, c_rst)
-        d_sc = v(V.tensor_tensor_scan(T.sc[:], T.rst[:], T.pm[:], -BIG, A.min, A.max))
-        sg, rl, fl, quant, fold, sums = {}, {}, {}, {}, {}, {}
-
-        def sign(m):
-            o = 512 * (31 - m)
-            sg[m] = s(S.activation(T.sg[:, o:o + 16 * m], T.pr[:, 0:16 * m], F.Sign, scale=-1.0, bias=T.sc[:, 16 * m + 15:16 * m + 16]))
-
-        def relu(m):
-            i, j, o = (0 if m > 28 else 1), (32 - m) % 4, 512 * (31 - m)
-            need("s", sg[m])
-            rl[m] = s(S.activation(T.ft[:, 4 * CO[i] + j:4 * CO[i] + 64 * m:4], T.sg[:, o:o + 16 * m], F.Relu, accum_out=T.rs[:, m:m + 1]))
-
-        def flags(i, js):
-            for j in js:
-                m = ROWS[i][j]
-                fl[i] = v(V.tensor_scalar(T.ft[:, 4 * CO[i] + j:4 * CO[i] + 64 * m:4], T.pp[:, 0:16 * m], T.sc[:, 16 * m + 15:16 * m + 16], None, A.is_lt))
-
-        def quantise(i, *d):
-            need("v", *d)
-            a, b = CO[i], CO[i] + NS[i]
-            quant[i] = v(V.quantize_mx(T.fq[:, a:b], T.fs[:, a:b], T.ft[:, 4 * a:4 * b]))
-
-        def folds(i):
-            need("p", quant[i], c_fq)
-            if i >= 5: need("p", sums[i - 3])
-            w = FOLD[i]
-            for k in range(2):
-                q, c = BANK[2 * ((i - 2) % 3) + k]
-                n = NS[i] // w
+        plan = PLAN[t]
+        N = lambda k: "%s@%d" % (k, t)
+        vs, ss, ps = plan["v"].split(), plan["s"].split(), plan["p"].split()
+        lo, hi = plan["pairs"]
+        nw = (hi - lo) // 2 + 1
+        have = [covering(plan, t, "x", 0, 16), covering(plan, t, "x", 16, 32)] if t else [[("lxa", 16)], [("lxb", 16)]]
+        sums = [N("odd")] + [N(k) for k in ss if k[0] == "d"]
+        signs = [k for k in ss if k[0] == "s"]
+        writer = {m: N(("r%d" if "r%d" % m in ss else "f%d") % m) for m in range(1, 32)}
+        writer[32] = N("dg")
+        folds = [int(k[1:]) for k in ps if k[0] == "o"]
+        bank = {m: BANK[n % len(BANK)] for n, m in enumerate(folds)}
+        before = {m: N("a%d" % folds[n - len(BANK)]) for n, m in enumerate(folds) if n >= len(BANK)}
+        tiles = [int(k[1:]) for k in ps if k[0] == "c"]
+        early = [k for k in vs[:vs.index("pmD")] if k[0] == "f" and k != "fq"]
+        part = {"A": (0, 256, T.pp, "sA"), "D": (256, 512, T.pe, "sB")}
+        held = lambda m: N("scA" if m < 16 else "scD")
+        col = lambda m: T.sc[:, 16 * m + 15:16 * m + 16]
+        rows = lambda m: T.ft[:, 4 * CO[slot(m)[0]] + slot(m)[1]:4 * CO[slot(m)[0]] + 64 * m:4]
+        listed = lambda k: N("lo%d" % (int(k.split("_")[1]) // 16))
+        for b in range(4):
+            gg(N("xp"), lambda b=b: g.affine_select(XP[:, 512 * b:512 * b + 512], X[:, b:2048:4], [[0, 512]], A.is_ge, 0.0, 0, 0), *(have[0] + have[1]))
+        for b in range(4 if t == 0 else 0):
+            gg("eb", lambda b=b: g.affine_select(T.eb[:, 512 * b:512 * b + 512], T.eighth[:], [[-1, 512]], A.is_equal, 0.0, b, 4), "c8")
+        for k in vs:
+            if k[0] == "_": v(k[1:], K[k[1:]][0], *K[k[1:]][1])
+            elif k[0] in "wx": head("v", k, t)
+            elif k[0] == "t": pick("v", k, N(k), T.st, XP, T.lo, 1.0, listed(k), N("xp"))
+            elif k == "e1": v(N(k), lambda: V.tensor_tensor_scan(T.e1[:], T.hk[:], T.pc[:], 0.0, A.mult, A.max), N("c%d" % tiles[-1]), "hk")
+            elif k == "a2": v(N(k), lambda: V.tensor_tensor(T.a2[:], T.a1[:], T.cr[:], A.add), N("a1"), N("cr"))
+            elif k == "a2b": v(N(k), lambda: V.tensor_tensor(T.a2b[:], T.a2[:], T.e1[:, 15:512:16], A.add), N("a2"), N("e1"))
+            elif k == "a3": v(N(k), lambda: V.tensor_tensor(T.a3[:], T.a2b[:], T.rs[:], A.subtract), N("a2b"), *sums)
+            elif k == "il": v(N(k), lambda: V.tensor_copy(T.il[:], T.a3[:]), N("a3"))
+            elif k == "inv": v(N(k), lambda: V.tensor_copy(T.inv[:, 0:512].indirect(T.il[:, 0:32]), T.iot[:]), N("il"), "iot")
+            elif k[:2] == "e2":
+                h = int(k[2])
+                v(N(k), lambda h=h: V.tensor_tensor_scan(T.e2[:, 256 * h:256 * h + 256], T.hk[:, 0:256], T.inv[:, 256 * h:256 * h + 256], 0.0, A.mult, A.max), N("inv"))
+            elif k[:2] == "lo":
+                h = int(k[2])
+                v(N(k), lambda h=h: V.tensor_scalar(T.lo[:, 16 * h:16 * h + 16], T.e2[:, 256 * h + 15:256 * h + 256:16], T.isc[:], -1.0, A.mult, A.add), N("e2%d" % h), "isc")
+            elif k[:2] == "sq":
+                h = int(k[2])
+                v(N(k), lambda h=h: V.quantize_mx(SQ[:, 256 * h:256 * h + 256], SS[:, 256 * h:256 * h + 256], T.st[:, 1024 * h:1024 * h + 1024]),
+                  *covering(plan, t, "t", 16 * h, 16 * h + 16))
+            elif k in ("qA", "qB"):
+                h = "AB".index(k[1])
+                v(N(k), lambda h=h: V.quantize_mx(XQ[:, 256 * h:256 * h + 256], XS[:, 256 * h:256 * h + 256], X[:, 1024 * h:1024 * h + 1024]), *have[h])
+            elif k == "fq":
+                v("fq", lambda: V.quantize_mx(T.fwq[:], T.fws[:], T.fw[:]), "fw0", "fw1", "fw2", "fw3")
+            elif k[:2] == "pm":
+                a, e, q, d = part[k[2]]
+                v(N(k), lambda a=a, e=e, q=q: V.tensor_tensor(T.pm[:, a:e], q[:, 0:256], T.maskb[:, a:e], A.min), N(d), "maskb")
+            elif k[:2] == "sc":
+                a, e = part[k[2]][:2]
+                v(N(k), lambda a=a, e=e: V.tensor_tensor_scan(T.sc[:, a:e], T.rst[:, a:e], T.pm[:, a:e], -BIG, A.min, A.max), N("pm" + k[2]), "rst")
+            elif k == "dg":
+                v(N(k), lambda: V.tensor_tensor(T.ft[:, 0:4 * C:4], T.pp[:], T.sc[:], A.is_le), N("sZ"), N("scA"), N("scD"), "z0")
+            elif k == "cum":
+                v(N(k), lambda: V.tensor_tensor_scan(T.cum[:], T.hold[:], T.ft[:, 0:4 * C:4], 0.0, A.mult, A.add), N("dg"), "hold")
+            elif k == "bq":
+                v("bq", lambda: V.quantize_mx(T.bq[:], T.bs[:], T.bt[:]), "b1")
+            elif k == "a1":
+                v(N(k), lambda: V.tensor_tensor(T.a1[:], T.ac0[:], T.cum[:, 15:512:16], A.subtract), N("cum"), "ac0")
+            elif k[0] == "f":
+                m = int(k[1:])
+                v(N(k), lambda m=m: V.tensor_scalar(rows(m), T.pp[:, 0:16 * m], col(m), None, A.is_lt), N("sA" if k in early else "sZ"), held(m), "z%d" % slot(m)[0])
+            else:
+                i = int(k[1:])
+                a, e = CO[i], CO[i] + NS[i]
+                v(N(k), lambda a=a, e=e: V.quantize_mx(T.fq[:, a:e], T.fs[:, a:e], T.ft[:, 4 * a:4 * e]), *[writer[32 - 4 * i - j] for j in range(4)])
+        for k in ss:
+            m = int(k[1:]) if k[0] in "srad" else 0
+            if k[0] == "_": s(k[1:], K[k[1:]][0], *K[k[1:]][1])
+            elif k[0] == "x": head("s", k, t)
+            elif k[0] == "t": pick("s", k, N(k), T.st, XP, T.lo, 1.0, listed(k), N("xp"))
+            elif k == "hk":
+                s("hk", lambda: S.activation(T.hk[:], T.hk1[:, 0:16].indirect(T.rep[:, 0:32]), F.Copy), "hk1", "rep")
+            elif k == "hw":
+                s(N("hw"), lambda: S.activation(T.hw[:, 0:nw], T.rs[:, lo:hi + 1:2], F.Copy, scale=1.0 / PK, bias=WHOLE), *[N("a%d" % m) for m in folds])
+                s(N("cr"), lambda: S.activation(T.cr[:, lo:hi + 1:2], T.hw[:, 0:nw], F.Copy, scale=PK, bias=-WHOLE * PK), N("hw"), "cr0")
+                s(N("odd"), lambda: S.activation(T.rs[:, lo - 1:hi:2], T.hw[:, 0:nw], F.Copy, bias=-WHOLE))
+            elif k[0] == "s":
+                o = 512 * signs.index(k)
+                src = T.pa[:, 1536:1536 + 16 * m] if m < 16 else T.pf[:, 0:16 * m]
+                s(N(k), lambda m=m, o=o, src=src: S.activation(T.sg[:, o:o + 16 * m], src, F.Sign, scale=-1.0, bias=col(m)), N("sX" if m < 16 else "sY"), held(m))
+            elif k[0] == "r":
+                o = 512 * signs.index("s%d" % m)
+                s(N(k), lambda m=m, o=o: S.activation(rows(m), T.sg[:, o:o + 16 * m], F.Relu, accum_out=T.rs[:, m:m + 1]), N("s%d" % m), "z%d" % slot(m)[0], "rs0")
+            elif k[0] == "a":
+                q, c = bank[m]
+                w = min(FOLD[slot(m)[0]], 16 * m)
+                jo = 112 * m
+                s(N(k), lambda m=m, q=q, c=c, w=w, jo=jo: S.activation(T.junk[:, jo:jo + w], q[:, c:c + w], F.Copy, accum_out=T.rs[:, m:m + 1]), N("o%d" % m), "rs0")
+            else:
+                s(N(k), lambda m=m: S.activation(T.junk[:, 128 * m - 128:144 * m - 128], rows(m), F.Copy, accum_out=T.rs[:, m:m + 1]), N("f%d" % m), "rs0")
+        for k in ps:
+            if k[0] == "s":
+                o, a, e, d = {"A": (T.pp[:, 0:256], 0, 256, [N("qA")]), "B": (T.pe[:, 0:256], 256, 512, [N("qB")]), "X": (T.pa[:, 1536:1792], 0, 256, [N("qA")]),
+                              "Y": (T.pf[:], 0, 512, [N("qA"), N("qB")]), "Z": (T.pp[:], 0, 512, [N("qB"), N("pmA")] + [N(f) for f in early])}[k[1]]
+                p(N(k), lambda o=o, a=a, e=e: P.matmul_mx(o, T.ur[:], T.urs[:], XQ[:, a:e], XS[:, a:e], True, True), "ur", "urs", *d)
+            elif k[0] == "o":
+                m = int(k[1:])
+                i, j = slot(m)
+                q, c = bank[m]
+                w = FOLD[i]
+                n = -(-16 * m // w)
+                d = [N("q%d" % i), "fq", N("pmD")] + ([before[m]] if m in before else [])
+                d += [N(z) for z in signs if int(z[1:]) < 16 and c == 1536]
                 for e in range(n):
                     a = CO[i] + w * e
-                    fold[i, k] = p(P.matmul_mx(q[:, c:c + w], T.fwq[:, 128 * k:128 * k + 128], T.fws[:, 128 * k:128 * k + 128], T.fq[:, a:a + w], T.fs[:, a:a + w], e == 0, e == n - 1))
-
-        def columns(i):
-            need("p", quant[i], c_bq)
-            return p(P.matmul_mx(T.pc[:, 0:NS[i]], T.bq[:], T.bs[:], T.fq[:, CO[i]:CO[i] + NS[i]], T.fs[:, CO[i]:CO[i] + NS[i]], i == 0, i == 1))
-
-        def along(i):
-            for k in range(2):
-                q, c = BANK[2 * ((i - 2) % 3) + k]
-                m = ROWS[i][2 * k]
-                w = min(FOLD[i], 16 * m)
-                jo = 192 * (2 * (i - 2) + k)
-                need("s", fold[i, k])
-                sums[i] = s(S.activation(T.junk[:, jo:jo + w], q[:, c:c + w], F.Copy, accum_out=T.rs[:, m:m + 1]))
-
-        need("s", d_sc, c_rs, z[-1], d_pr)
-        need("v", d_sc, d_pr, *z)
-        sign(31); sign(30); relu(31); sign(29); relu(30); sign(28); relu(29)
-        flags(2, range(4))
-        d_dg = v(V.tensor_tensor(T.ft[:, 0:4 * C:4], T.pp[:], T.sc[:], A.is_le))
-        quantise(2, fl[2])
-        folds(2)
-        flags(3, range(4))
-        if t == 0:
-            need("v", k_b1)
-            c_bq = v(V.quantize_mx(T.bq[:], T.bs[:], T.bt[:]))
-        need("v", d_dg, c_hold)
-        d_cum = v(V.tensor_tensor_scan(T.cum[:], T.hold[:], T.ft[:, 0:4 * C:4], 0.0, A.mult, A.add))
-        quantise(3, fl[3])
-        folds(3)
-        relu(28); along(2); sign(27); sign(26); relu(27); along(3); sign(25); relu(26); relu(25)
-        quantise(0, d_dg, rl[29])
-        columns(0); columns(2); columns(3)
-        flags(4, range(4))
-        flags(5, [0])
-        quantise(4, fl[4])
-        folds(4); columns(4)
-        flags(5, [1, 2, 3])
-        flags(6, [0])
-        quantise(5, fl[5])
-        folds(5); columns(5)
-        along(4); along(5)
-        flags(6, [1, 2, 3])
-        flags(7, range(4))
-        quantise(6, fl[6])
-        quantise(7, fl[7])
-        quantise(1, rl[25])
-        folds(6); folds(7); columns(6); columns(7)
-        d_pc = columns(1)
-        along(6); along(7)
-        need("s", sums[7], c_cr)
-        d_hw = s(S.activation(T.hw[:], T.rs[:, 2:25:2], F.Copy, scale=1.0 / PK, bias=WHOLE))
-        need("s", d_hw)
-        d_odd = s(S.activation(T.rs[:, 1:24:2], T.hw[:], F.Copy, bias=-WHOLE))
-        d_cr = s(S.activation(T.cr[:, 2:25:2], T.hw[:], F.Copy, scale=PK, bias=-WHOLE * PK))
-        need("v", d_cum, c_ac0)
-        d_a1 = v(V.tensor_tensor(T.a1[:], T.ac0[:], T.cum[:, 15:512:16], A.subtract))
-        need("v", d_pc, c_hk)
-        d_e1 = v(V.tensor_tensor_scan(T.e1[:], T.hk[:], T.pc[:], 0.0, A.mult, A.max))
-        need("v", d_a1, d_odd)
-        d_a2 = v(V.tensor_tensor(T.a2[:], T.a1[:], T.rs[:], A.subtract))
-        need("v", d_e1, c_isc)
-        d_a2s = v(V.tensor_scalar(T.a2s[:], T.e1[:, 15:512:16], T.isc[:], None, A.mult))
-        need("v", d_a2, d_cr)
-        d_a2 = v(V.tensor_tensor(T.a2b[:], T.a2[:], T.cr[:], A.add))
-        need("v", d_a2, d_a2s)
-        d_a3 = v(V.tensor_tensor(T.a3[:], T.a2b[:], T.a2s[:], A.add))
-        need("v", d_a3)
-        d_il = v(V.tensor_copy(T.il[:], T.a3[:]))
-        need("v", d_il, k_io)
-        d_inv = v(V.tensor_copy(T.inv[:, 0:512].indirect(T.il[:, 0:32]), T.iot[:]))
-        need("v", d_inv)
-        d_e2 = v(V.tensor_tensor_scan(T.e2[:], T.hk[:], T.inv[:], 0.0, A.mult, A.max))
-        need("v", d_e2, c_isc4)
-        dl = {}
-        for i in (2, 0, 3, 1):
-            dl[i] = v(V.tensor_scalar(T["l%d" % i][:], T.e2[:, 15:512:16], T.isc4[:], float(i - 4), A.mult, A.add))
+                    p(N(k), lambda q=q, c=c, w=w, a=a, e=e, n=n, j=j: P.matmul_mx(q[:, c:c + w], T.fwq[:, 64 * j:64 * j + 128], T.fws[:, 64 * j:64 * j + 128],
+                                                                                T.fq[:, a:a + w], T.fs[:, a:a + w], e == 0, e == n - 1), *d)
+            else:
+                i = int(k[1:])
+                p(N(k), lambda i=i: P.matmul_mx(T.pc[:, 0:NS[i]], T.bq[:], T.bs[:], T.fq[:, CO[i]:CO[i] + NS[i]], T.fs[:, CO[i]:CO[i] + NS[i]], i == tiles[0], i == tiles[-1]),
+                  N("q%d" % i), "bq")
         for h in range(2):
-            o = {}
-            for i in (2, 3):
-                need("s", dl[i])
-                o[i] = s(S.activation(T.st[:, 1024 * h + i:1024 * h + 1024:4], X[:, 0:2048].indirect(T["l%d" % i][:, 16 * h:16 * h + 16]), F.Copy))
-            for i in (0, 1):
-                need("v", dl[i])
-                o[i] = v(V.tensor_copy(T.st[:, 1024 * h + i:1024 * h + 1024:4], X[:, 0:2048].indirect(T["l%d" % i][:, 16 * h:16 * h + 16])))
-            need("v", *o.values())
-            d_q = v(V.quantize_mx(SQ[:, 256 * h:256 * h + 256], SS[:, 256 * h:256 * h + 256], T.st[:, 1024 * h:1024 * h + 1024]))
-            need("g", d_q)
+            d_q = N("sq%d" % h)
             blocks = [4 * h + k for k in range(4)]
             for kind in range(2):
                 tr, k = [], 0
@@ -321,112 +341,103 @@ def rank_program(g, core, T, topo):
                     if kind == 0: sv, dv = SQ[:, BL * b:BL * b + BL].bitcast(dt.uint8), LC[:, BL * rank:BL * rank + BL].bitcast(dt.uint8)
                     else: sv, dv = SS[:, BL * b:BL * b + BL], LS[:, BL * rank:BL * rank + BL]
                     tr.append(put(sv, [r], dv, "sa%d_%d" % (t, rank), es))
-                g.remote_dma_fused(tr, local_sem=sem.lsem)
+                raw("g", lambda tr=tr: g.remote_dma_fused(tr, local_sem=sem.lsem), d_q)
             if own in blocks:
-                need("y", d_q)
-                Y.dma_start(LC[:, BL * rank:BL * rank + BL].bitcast(dt.uint8), SQ[:, BL * own:BL * own + BL].bitcast(dt.uint8)).then_inc(sem["cs%d" % t], 16)
-                Y.dma_start(LS[:, BL * rank:BL * rank + BL], SS[:, BL * own:BL * own + BL]).then_inc(sem["cs%d" % t], 16)
+                raw("y", lambda: Y.dma_start(LC[:, BL * rank:BL * rank + BL].bitcast(dt.uint8), SQ[:, BL * own:BL * own + BL].bitcast(dt.uint8)).then_inc(sem["cs%d" % t], 16), d_q)
+                raw("y", lambda: Y.dma_start(LS[:, BL * rank:BL * rank + BL], SS[:, BL * own:BL * own + BL]).then_inc(sem["cs%d" % t], 16))
         if t == 0:
-            need("v", k_eb)
-            c_eq = v(V.quantize_mx(T.eq[:], T.es[:], T.eb[:]))
-            c_mt = v(V.memset(T.mt[:], 0.0))
-            c_ht = v(V.memset(T.ht[:], 0.0))
-            need("v", c_mt)
-            for w in range(R): pad = v(V.quantize_mx(T["lc%d" % w][:, 512:640], T["ls%d" % w][:, 512:640], T.mt[:]))
-        d_sh = v(V.tensor_scalar(T.sh[:], T.st[:], 0.125, None, A.mult))
+            v("eq", lambda: V.quantize_mx(T.eq[:], T.es[:], T.eb[:]), "eb")
+            v("mt", lambda: V.memset(T.mt[:], 0.0))
+            v("ht", lambda: V.memset(T.ht[:], 0.0))
+            for w in range(R): v("pad", lambda w=w: V.quantize_mx(T["lc%d" % w][:, 512:640], T["ls%d" % w][:, 512:640], T.mt[:]), "mt")
+        v(N("sh"), lambda: V.tensor_scalar(T.sh[:], T.st[:], 0.125, None, A.mult))
         if last:
-            d_ol = v(V.tensor_scalar(T.olt[:], T.inv[:], -1.0, None, A.add))
-            need("v", ("lv", 16))
-            c_vq = v(V.quantize_mx(T.vq[:], T.vsc[:], T.vt[:]))
-        need("p", d_q, c_eq)
+            v("ol", lambda: V.tensor_scalar(T.olt[:], T.inv[:], -1.0, None, A.add))
+            v("vq", lambda: V.quantize_mx(T.vq[:], T.vsc[:], T.vt[:]), ("lv", 16))
+            raw("y", lambda: Y.dma_start(T.ol[:, :], T.olt[0:128:16, :]).then_inc(sem.so, 16), "ol")
         arrived = lambda r: ("cs%d" % t, 32) if r == rank else ("sa%d_%d" % (t, r), 2 * len(ne) if r in mate else 4)
         E = lambda b: (T.eq[:, 128 * b:128 * b + 128], T.es[:, 128 * b:128 * b + 128])
-        part = {(0, b): (T.pa, 512 * b) for b in (1, 2, 3)}
-        part.update({(1, 1): (T.pp, 0), (1, 2): (T.pc, 0), (1, 3): (T.pe, 0)})
-
-        def in_bank(r):
-            if r == 7: need("p", pad)
-            return p(P.matmul_mx(T.pa[:, 0:128], *E(0), LC[:, BL * r:BL * r + 128], LS[:, BL * r:BL * r + 128], r == 0, r == 7))
-
-        d_u = {}
-        for h in range(2):
-            for r in range(4): need("p", arrived(4 * h + r))
-            for b in (1, 2, 3):
-                q, c = part[h, b]
-                d_u[h, b] = p(P.matmul_mx(q[:, c:c + 256], *E(b), LC[:, 256 * h:256 * h + 256], LS[:, 256 * h:256 * h + 256], True, True))
-            for r in ((0, 1, 2) if h == 0 else (3, 4, 5, 6, 7)): d_m0 = in_bank(r)
-        acc = {}
-        for b in (1, 2, 3):
-            need("s", d_u[0, b])
-            acc[b] = s(S.activation(T.acb[:, 64 * (b - 1):64 * b], T.pa[:, 512 * b:512 * b + 64], F.Copy))
-        need("v", c_mt)
-        for r in range(1, 8):
-            for b in (1, 2, 3):
-                q, c = part[r // 4, b]
-                c += 64 * (r % 4)
-                need("v", d_u[r // 4, b], acc[b])
-                out = T.acb[:, 64 * (b - 1):64 * b] if r < 7 else T.mt[:, b:256:4]
-                acc[b] = v(V.tensor_tensor(out, q[:, c:c + 64], T.acb[:, 64 * (b - 1):64 * b], A.add))
-        need("s", d_m0, c_mt)
-        d = s(S.activation(T.mt[:, 0:256:4], T.pa[:, 0:64], F.Copy))
-        need("v", d, *acc.values())
-        d_mq = v(V.quantize_mx(T.mq[:], T.ms[:], T.mt[:]))
-        need("p", d_mq, ("lw", 16), ("lws", 16))
-        d_h = [p(P.matmul_mx(T.pa[:, 512 * b:512 * b + 128], T.wq[:, 128 * b:128 * b + 128], T.wsc[:, 128 * b:128 * b + 128], T.mq[:], T.ms[:], True, True)) for b in range(4)]
-        o = []
+        wait = [d_q, "eq", "pad"] + [arrived(r) for r in range(8)]
+        side = {b: q for b, q in zip(SIDE, (T.pp, T.pc))}
+        for b in SIDE:
+            p(N("u%d" % b), lambda b=b: P.matmul_mx(side[b][:, 0:C - BL * KP], *E(b), LC[:, BL * KP:C], LS[:, BL * KP:C], True, True), *wait)
+            s(N("k%d" % b), lambda b=b: S.activation(T.acb[:, BL * b:BL * b + BL], side[b][:, 0:BL], F.Copy), N("u%d" % b))
+        for b in list(SIDE) + [b for b in range(4) if b not in SIDE]:
+            n = KP if b in SIDE else 8
+            for r in range(n):
+                p(N("m%d" % b), lambda r=r, b=b, n=n: P.matmul_mx(T.pa[:, 512 * b:512 * b + 128], *E(b), LC[:, BL * r:BL * r + 128], LS[:, BL * r:BL * r + 128], r == 0, r == n - 1), *wait)
+        for r in range(KP, 8):
+            for b in SIDE:
+                x = T.pa[:, 512 * b:512 * b + BL] if r == KP else side[b][:, BL * (r - KP):BL * (r - KP + 1)]
+                out = T.acb[:, BL * b:BL * b + BL] if r < 7 else T.mt[:, b:256:4]
+                v(N("acc%d%d" % (r, b)), lambda x=x, out=out, b=b: V.tensor_tensor(out, x, T.acb[:, BL * b:BL * b + BL], A.add),
+                  *([N("m%d" % b), N("k%d" % b), "mt"] if r == KP else [N("acc%d%d" % (r - 1, b))]))
         for b in range(4):
-            need("s" if b % 2 == 0 else "v", d_h[b], c_ht)
-            if b % 2 == 0: o.append(s(S.activation(T.ht[:, b:256:4], T.pa[:, 512 * b:512 * b + 64], F.Relu, scale=0.0625)))
-            else: o.append(v(V.tensor_scalar(T.ht[:, b:256:4], T.pa[:, 512 * b:512 * b + 64], 0.0, 0.0625, A.max, A.mult)))
-        need("v", *o)
-        d_hq = v(V.quantize_mx(HQ[:], HS[:], T.ht[:]))
-        need("g", d_hq)
+            if b not in SIDE: s(N("acc7%d" % b), lambda b=b: S.activation(T.mt[:, b:256:4], T.pa[:, 512 * b:512 * b + 64], F.Copy), N("m%d" % b), "mt")
+        v(N("mq"), lambda: V.quantize_mx(T.mq[:], T.ms[:], T.mt[:]), *[N("acc7%d" % b) for b in range(4)])
+        for b in range(4):
+            p(N("h%d" % b), lambda b=b: P.matmul_mx(T.pa[:, 512 * b:512 * b + 128], T.wq[:, 128 * b:128 * b + 128], T.wsc[:, 128 * b:128 * b + 128], T.mq[:], T.ms[:], True, True),
+              N("mq"), ("lw", 16), ("lws", 16))
+            if b % 2 == 0: s(N("re%d" % b), lambda b=b: S.activation(T.ht[:, b:256:4], T.pa[:, 512 * b:512 * b + 64], F.Relu, scale=0.0625), N("h%d" % b), "ht")
+            else: v(N("re%d" % b), lambda b=b: V.tensor_scalar(T.ht[:, b:256:4], T.pa[:, 512 * b:512 * b + 64], 0.0, 0.0625, A.max, A.mult), N("h%d" % b), "ht")
+        d_hq = v(N("hq"), lambda: V.quantize_mx(HQ[:], HS[:], T.ht[:]), *[N("re%d" % b) for b in range(4)])
         hsem = ["ha%d" % t, "hb%d" % t]
         for kind in range(2):
             if kind == 0: sv, dv = HQ[:, 0:BL].bitcast(dt.uint8), HL[:, BL * own:BL * own + BL].bitcast(dt.uint8)
             else: sv, dv = HS[:, 0:BL], HP[:, BL * own:BL * own + BL]
-            g.remote_dma_fused([put(sv, far, dv, hsem[own // 4], fe), put(sv, mate, dv, hsem[own // 4], ne)], local_sem=sem.lsem)
-        need("y", d_hq)
-        Y.dma_start(HL[:, BL * own:BL * own + BL].bitcast(dt.uint8), HQ[:, 0:BL].bitcast(dt.uint8)).then_inc(sem["ch%d" % t], 16)
-        Y.dma_start(HP[:, BL * own:BL * own + BL], HS[:, 0:BL]).then_inc(sem["ch%d" % t], 16)
-        if last:
-            need("y", d_ol)
-            Y.dma_start(T.ol[:, :], T.olt[0:128:16, :]).then_inc(sem.so, 16)
-        need("p", d_hq)
-        add = {}
+            tr = [put(sv, far, dv, hsem[own // 4], fe), put(sv, mate, dv, hsem[own // 4], ne)]
+            raw("g", lambda tr=tr: g.remote_dma_fused(tr, local_sem=sem.lsem), d_hq)
+        raw("y", lambda: Y.dma_start(HL[:, BL * own:BL * own + BL].bitcast(dt.uint8), HQ[:, 0:BL].bitcast(dt.uint8)).then_inc(sem["ch%d" % t], 16), d_hq)
+        raw("y", lambda: Y.dma_start(HP[:, BL * own:BL * own + BL], HS[:, 0:BL]).then_inc(sem["ch%d" % t], 16))
         for h in range(2):
             rs = [r for r in ow[4 * h:4 * h + 4] if r != rank]
-            need("p", (hsem[h], 2 * sum(len(ne) if r in mate else len(fe) for r in rs)))
-            if own // 4 == h: need("p", ("ch%d" % t, 32))
-            bank = [(T.pa, 512 * b) for b in range(4)] if h == 0 else [(T.pp, 0), (T.pc, 0), (T.pe, 0), (T.pf, 0)]
-            for b in (0, 1, 3, 2):
-                q, c = bank[b]
-                d = p(P.matmul_mx(q[:, c:c + 256], *E(b), HL[:, 256 * h:256 * h + 256], HP[:, 256 * h:256 * h + 256], True, True))
-                need("v", d, d_sh)
-                a = 512 * b + 256 * h
-                add[b] = v(V.tensor_tensor(T.sn[:, a:a + 256], q[:, c:c + 256], T.sh[:, 1024 * h + b:1024 * h + 1024:4], A.add))
-        o = []
-        for q, b, a, e in (("s", 0, 0, 2), ("s", 1, 0, 2), ("v", 3, 0, 2), ("s", 2, 0, 1), ("v", 2, 1, 2)):
-            need(q, add[b])
-            w, out = T.sn[:, 512 * b:512 * b + 512].indirect(T.il[:, 16 * a:16 * e]), XN[:, 1024 * a + b:1024 * e:4]
-            if q == "s": o.append(s(S.activation(out, w, F.Copy, scale=4.0)))
-            else: o.append(v(V.tensor_scalar(out, w, 4.0, None, A.mult)))
-        need("v", *o)
-        xq = v(V.quantize_mx(T["xq%d" % (t + 1)][:], T["xs%d" % (t + 1)][:], XN[:]))
+            d = [d_hq, (hsem[h], 2 * sum(len(ne) if r in mate else len(fe) for r in rs))]
+            if own // 4 == h: d.append(("ch%d" % t, 32))
+            at = [(T.pa, 512 * b) for b in range(4)] if h == 0 else [(T.pp, 0), (T.pc, 0), (T.pe, 0), (T.pf, 0)]
+            for b in range(4):
+                q, c = at[b]
+                p(N("d%d%d" % (h, b)), lambda q=q, c=c, b=b, h=h: P.matmul_mx(q[:, c:c + 256], *E(b), HL[:, 256 * h:256 * h + 256], HP[:, 256 * h:256 * h + 256], True, True), *d)
+                if h == 0:
+                    v(N("add%d" % b), lambda q=q, c=c, b=b: V.tensor_tensor(T.sn[:, 512 * b:512 * b + 256], q[:, c:c + 256], T.sh[:, b:1024:4], A.add), N("d0%d" % b), N("sh"))
 
-    XQ, XS = T["xq%d" % R], T["xs%d" % R]
-    need("y", xq)
-    Y.dma_start(T.oc[:, :], XQ[:].bitcast(dt.uint8)).then_inc(sem.so, 16)
-    for k in range(4): Y.dma_start(T.osc[4 * k:4 * k + 4, :], XS[32 * k:32 * k + 4, :]).then_inc(sem.so, 16)
-    need("p", xq, c_vq)
-    d_y = [p(P.matmul_mx(b[:, 0:256], T.vq[:], T.vsc[:], XQ[:, 256 * k:256 * k + 256], XS[:, 256 * k:256 * k + 256], True, True)) for k, b in enumerate((T.pp, T.pc))]
-    need("v", d_y[0])
-    y0 = v(V.tensor_copy(T.yt[:, 0:256], T.pp[:, 0:256]))
-    need("s", d_y[1])
-    y1 = s(S.activation(T.yt[:, 256:512], T.pc[:, 0:256], F.Copy))
-    need("g", y0)
-    g.wait_ge(sem.lsem, local[0])
-    need("s", y0, y1)
-    S.dma_start(T.y[:, :], T.yt[:, :]).then_inc(sem.sy, 16)
-    need("s", ("sy", 16))
-    need("y", *[(k, n) for k, n in cnt.items()], ("so", 16 * 6))
+    for t in range(R): one_round(t)
+    plan = PLAN[R]
+    XN, XQ2, XS2 = T["x%d" % R], T["xq%d" % R], T["xs%d" % R]
+    cuts = plan["cuts"]
+    n = len(cuts) - 1
+    for q in "vs":
+        for k in plan[q].split():
+            if k[0] in "wx":
+                head(q, k, R)
+                continue
+            j = int(k[1])
+            a, e = 16 * cuts[j], 16 * cuts[j + 1]
+            if k[0] == "q": v(k, lambda a=a, e=e: V.quantize_mx(XQ2[:, a:e], XS2[:, a:e], XN[:, 4 * a:4 * e]), *covering(plan, R, "x", cuts[j], cuts[j + 1]))
+            elif k[0] == "y" and q == "s": s(k, lambda a=a, e=e, j=j: S.activation(T.yt[:, a:e], T.pa[:, 512 * j:512 * j + e - a], F.Copy), "py%d" % j)
+            elif k[0] == "y": v(k, lambda a=a, e=e, j=j: V.tensor_copy(T.yt[:, a:e], T.pa[:, 512 * j:512 * j + e - a]), "py%d" % j)
+            else: raw("s", lambda a=a, e=e: S.dma_start(T.y[:, a:e], T.yt[:, a:e]).then_inc(sem.so, 16), "y%d" % j)
+    for j in range(n):
+        a, e = 16 * cuts[j], 16 * cuts[j + 1]
+        p("py%d" % j, lambda a=a, e=e, j=j: P.matmul_mx(T.pa[:, 512 * j:512 * j + e - a], T.vq[:], T.vsc[:], XQ2[:, a:e], XS2[:, a:e], True, True), "q%d" % j, "vq")
+    for k in plan["y"].split():
+        j = int(k[1])
+        if k[0] == "O":
+            raw("y", lambda j=j: Y.dma_start(T.osc[4 * j:4 * j + 4, :], XS2[32 * j:32 * j + 4, :]).then_inc(sem.so, 16), "q%d" % (n - 1))
+            continue
+        a, e = 16 * cuts[j], 16 * cuts[j + 1]
+        if k[0] == "C": raw("y", lambda a=a, e=e: Y.dma_start(T.oc[:, 4 * a:4 * e], XQ2[:, a:e].bitcast(dt.uint8)).then_inc(sem.so, 16), "q%d" % j)
+        else: raw("y", lambda a=a, e=e: Y.dma_start(T.y[:, a:e], T.yt[:, a:e]).then_inc(sem.so, 16), "y%d" % j)
+    raw("g", None, ("lsem", local[0]))
+    raw("y", None, ("so", 16 * (2 * n + 5)), *[(SEM[q], count[q]) for q in SEM])
+
+    for q in Q:
+        seen = {}
+        for fn, deps, counted in calls[q]:
+            for d in deps:
+                k, n = named[d] if isinstance(d, str) else d
+                if seen.get(k, 0) < n:
+                    Q[q].wait_ge(sem[k], n)
+                    seen[k] = n
+            if fn is None: continue
+            inst = fn()
+            if counted: inst.then_inc(sem[SEM[q]], 1)

import numpy as np
from concourse.bass import DstId, RemoteDMATransfer
from concourse.mybir import dt, AluOpType as A, ActivationFunctionType as F

R = 2
C = 512
BL = 64
NS = [512, 448, 384, 320, 256, 192, 128, 128]
CO = [sum(NS[:s]) for s in range(8)]
FC = sum(NS)
FOLD = {1: 224, 2: 128, 3: 160, 4: 128, 5: 192, 6: 128}
BIG = 2.0 ** 94
PK = 1024.0
WHOLE = 1.5 * 2.0 ** 23
KP, SIDE = 4, (2, 3)

PLAN = [
    {"v": "_c8 _z1 _z2 _p1 _rs0 _z0 _z7 _pi _z4 _z6 _z5 _hk0 _uoff _z3 _rst _uq _p15 _rep _bn _hk2 _ur qA _ac0 _cr0 qB _hk1 _isc pmA pmD fq scD scA f19 f4 f17 f22 f23 f18 "
          "f21 f3 f20 f24 f15 f1 q2 bq f16 dg q3 f9 q0 f13 f14 f11 f12 q4 f5 q5 f2 f7 f8 f6 q7 cum q6 q1 a1 e1 a2 a2b a3 il inv e20 lo0 e21 t0_0_16 lo1 t3_0_16 t2_16_24 "
          "sq0 t1_16_32 sq1",
     "s": "_fw01 _fw00 _off _dja _maskb _urs _hold _fw1 _fw0 _fw2 _fw3 hk s29 s28 s30 s27 r29 s31 s26 s10 r31 r30 s25 r10 d4 r26 a22 a24 r28 r25 a20 r27 a14 a18 a12 a10 "
          "a16 a6 a8 d2 hw d1 d3 t2_0_16 t1_0_16 t3_16_32 t2_24_32 t0_16_32",
     "p": "sA sB sZ sY sX o24 o22 o20 o18 c0 c3 c2 o14 c5 o12 o10 c4 c7 o16 o6 c6 o8 c1",
     "pairs": (6, 24)},
    {"v": "w0 w1 w2 w3 x1_6_16 x3_0_10 qA x2_22_28 pmA x2_16_22 scA qB f14 f10 pmD scD f9 f16 f22 f23 f21 q4 dg f24 q5 f17 q2 f5 f18 f20 q0 f19 f25 q3 f6 f8 f26 q6 f2 f4 "
          "q1 f3 f1 cum q7 a1 e1 a2 a2b a3 il inv e20 lo0 e21 t0_0_16 lo1 t3_0_16 t2_16_24 sq0 t1_16_32 sq1",
     "s": "x0_0_16 x1_0_6 x2_0_16 x3_10_16 x1_16_32 x2_28_32 x3_16_32 x0_16_32 s11 s12 s15 s13 r15 r12 r11 s31 r13 s29 s7 s30 r29 r30 r31 s27 a16 r7 a10 a14 a22 s28 r27 "
          "r28 a24 a12 a18 a8 a6 a20 a26 d1 hw d2 d4 d3 t2_0_16 t1_0_16 t3_16_32 t2_24_32 t0_16_32",
     "p": "sA sX sB sZ sY o16 o10 o22 o14 o24 o12 c0 c2 c4 c5 c3 o18 o20 o6 o8 c6 o26 c1 c7",
     "pairs": (6, 26)},
    {"v": "w0 w1 w2 w3 x2_0_16 x3_0_24 x2_24_32 q0 q1 y1",
     "s": "x0_0_24 x1_0_24 x2_16_24 x1_24_32 x3_24_32 x0_24_32 y0 Y1",
     "y": "C0 O2 C1 O3 O1 O0 Y0",
     "cuts": [0, 24, 32]},
]

E4, U8, BF, F32, I32, U16 = "float8_e4m3fn_x4", "uint8", "bfloat16", "float32", "int32", "uint16"
SCRATCH = {}


def _sb(n, ty, *names):
    for k in names: SCRATCH[k] = ("sbuf", [128, n], ty)


def _mx(n, *pairs):
    for a, b in pairs:
        _sb(n, E4, a)
        _sb(n, U8, b)


_sb(2048, BF, "x0", "x1", "x2", "xp0", "xp1", "st", "sh", "sn", "eb")
_sb(16 * 224, F32, "junk")
_sb(512, BF, "ut", "vt", "bt", "bt2", "bw", "eighth", "mt", "ht", "c0", "off", "maskb", "rst", "hold", "hk", "cum")
_sb(1024, BF, "fw")
_sb(128, BF, "dj", "dja")
_sb(16, BF, "hk0", "hk1", "hk2", "bm")
_sb(11 * 512, BF, "sg")
_sb(4 * FC, BF, "ft")
_sb(512, F32, "iot", "pm", "sc", "e1", "e2", "inv", "olt", "yt")
_sb(256, F32, "acb")
_sb(32, F32, "m0", "ac0", "rs", "cr", "a1", "a2", "a2b", "a3")
_sb(16, F32, "hw")
_sb(1, F32, "pi", "p15", "isc")
_sb(1, I32, "p0", "p1")
_sb(8, I32, "uo0")
_sb(8, U16, "uoff")
_sb(32, U16, "il", "lo", "rep")
_mx(128, ("uq", "us"), ("ur", "urs"), ("vq", "vsc"), ("bq", "bs"), ("mq", "ms"), ("hq0", "hs0"), ("hq1", "hs1"))
_mx(256, ("fwq", "fws"))
_mx(512, ("wq", "wsc"), ("eq", "es"), ("xq0", "xs0"), ("xq1", "xs1"), ("xq2", "xs2"), ("sq0", "ss0"), ("sq1", "ss1"), ("hl0", "hp0"), ("hl1", "hp1"))
_mx(640, ("lc0", "ls0"), ("lc1", "ls1"))
_mx(FC, ("fq", "fs"))
SCRATCH.update({"pp": ("psum", [128, 512], F32), "pc": ("psum", [128, 512], F32), "pe": ("psum", [128, 512], F32), "pf": ("psum", [128, 512], F32),
                "pa": ("psum", [128, 2048], F32)})
SEMAPHORES = ["vs", "ss", "ps", "gs", "lxa", "lxb", "lu", "lv", "lw", "lws", "lsem", "so"]
SEMAPHORES += ["sa%d_%d" % (t, r) for t in range(R) for r in range(8)] + ["%s%d" % (k, t) for t in range(R) for k in ("ha", "hb", "cs", "ch")]


def owners(T, topo):
    by = {}
    for r, c in enumerate(T.cores): by.setdefault(topo.chip(c), []).append(r)
    first, second = [], []
    for k, ch in enumerate(sorted(by)):
        first.append(by[ch][k % 2])
        second.append(by[ch][1 - k % 2])
    return first + second


def slot(m):
    return (32 - m) // 4, (32 - m) % 4


def rank_program(g, core, T, topo):
    rank = T.rank_of(core)
    if rank is None: return
    sem = T.sem
    V, S, P, Y = g.vector, g.scalar, g.tensor, g.sync
    Q = {"g": g, "v": V, "s": S, "p": P, "y": Y}
    SEM = {"v": "vs", "s": "ss", "p": "ps", "g": "gs"}
    calls = {q: [] for q in Q}
    count = {q: 0 for q in SEM}
    named = {}

    def op(q, name, fn, *deps):
        count[q] += 1
        named[name] = (SEM[q], count[q])
        calls[q].append((fn, deps, True))
        return name

    def raw(q, fn, *deps):
        calls[q].append((fn, deps, False))

    def v(*a): return op("v", *a)
    def s(*a): return op("s", *a)
    def p(*a): return op("p", *a)
    def gg(*a): return op("g", *a)

    raw("s", lambda: S.dma_start(T.ut[:], T.u[:, :]).then_inc(sem.lu, 16))
    raw("y", lambda: Y.dma_start(T.x0[:, 0:1024], T.x[:, 0:1024]).then_inc(sem.lxa, 16))
    raw("y", lambda: Y.dma_start(T.x0[:, 1024:2048], T.x[:, 1024:2048]).then_inc(sem.lxb, 16))
    raw("y", lambda: Y.dma_start(T.wq[:].bitcast(dt.uint8), T.wc[:, :]).then_inc(sem.lw, 16), ("lxa", 16), ("lxb", 16))
    raw("y", lambda: Y.dma_start(T.wsc[:], T.ws[:, :]).then_inc(sem.lws, 16))
    raw("y", lambda: Y.dma_start(T.vt[:], T.v[:, :]).then_inc(sem.lv, 16))

    small = {"allow_small_or_imprecise_dtypes": True}
    gg("p0", lambda: g.iota(T.p0[:], [[0, 1]], 0, 1))
    gg("c0", lambda: g.iota(T.c0[:], [[0, 32], [1, 16]], 0, 0, **small))
    gg("uo0", lambda: g.iota(T.uo0[:], [[16, 8]], 0, 0))
    gg("dj", lambda: g.iota(T.dj[:], [[1, 128]], 0, -1, **small))
    gg("m0", lambda: g.iota(T.m0[:], [[16, 32]], 15, 0, **small))
    gg("one", lambda: g.iota(T.bt2[:], [[0, 512]], 1, 0, **small))
    gg("bw", lambda: g.affine_select(T.bw[:], T.bt2[:], [[0, 8], [1, 16], [0, 4]], A.is_equal, 2.0 ** -10, -15, 0), "one")
    gg("b0", lambda: g.affine_select(T.bt2[:], T.bw[:], [[-16, 8], [0, 64]], A.is_ge, 0.0, 0, 1), "bw")
    gg("b1", lambda: g.affine_select(T.bt[:], T.bt2[:], [[16, 8], [0, 64]], A.is_ge, 0.0, 15, -1), "b0")
    gg("iot", lambda: g.iota(T.iot[:], [[1, 512]], 1, 0, **small))
    K = {}

    def const(name, fn, *deps): K[name] = (fn, deps)

    const("c8", lambda: V.memset(T.eighth[:], 0.125))
    for i in range(8):
        w = 48 if i < 7 else 112
        const("z%d" % i, lambda i=i, w=w: V.memset(T.ft[:, 4 * (CO[i] + NS[i] - w):4 * (CO[i] + NS[i])], 0.0))
    const("cr0", lambda: V.memset(T.cr[:], 0.0))
    const("rs0", lambda: V.memset(T.rs[:], 0.0))
    const("rst", lambda: V.tensor_scalar(T.rst[:], T.c0[:], -0.5, 2.0 * BIG, A.add, A.mult), "c0")
    const("p1", lambda: V.tensor_scalar(T.p1[:], T.p0[:], 15, None, A.bitwise_and), "p0")
    const("uoff", lambda: V.tensor_copy(T.uoff[:], T.uo0[:]), "uo0")
    const("pi", lambda: V.tensor_scalar(T.pi[:], T.p1[:], -1.0, None, A.mult), "p1")
    const("uq", lambda: V.quantize_mx(T.uq[:], T.us[:], T.ut[:]), ("lu", 16))
    const("ur", lambda: V.tensor_copy(T.ur[:, 0:128].bitcast(dt.uint32), T.uq[:, 0:128].bitcast(dt.uint32).indirect(T.uoff[:, 0:8])), "uq", "uoff")
    const("hk0", lambda: V.tensor_scalar(T.hk0[:], T.c0[:, 0:16], T.pi[:], 1.0, A.add, A.is_equal), "pi", "c0")
    const("hk2", lambda: V.tensor_scalar(T.hk2[:], T.hk0[:], 1023.0, 1.0, A.mult, A.add), "hk0")
    const("hk1", lambda: V.tensor_tensor(T.hk1[:], T.hk2[:], T.bm[:, 0:16], A.mult), "hk2", "bn")
    const("bn", lambda: V.tensor_scalar(T.bm[:, 0:16], T.c0[:, 0:16], T.pi[:], 0.0, A.add, A.not_equal), "pi", "c0")
    const("rep", lambda: V.tensor_scalar(T.rep[:], T.m0[:], 0.0, T.pi[:], A.mult, A.subtract), "m0", "pi")
    const("ac0", lambda: V.tensor_scalar(T.ac0[:], T.m0[:], T.pi[:], None, A.add), "m0", "pi")
    const("p15", lambda: V.tensor_scalar(T.p15[:], T.p1[:], 15.0, 1.0 - 2.0 ** -10, A.is_equal, A.mult), "p1")
    const("isc", lambda: V.tensor_scalar(T.isc[:], T.p15[:], 2.0 ** -10, None, A.add), "p15")
    for k in range(2): const("fw0%d" % k, lambda k=k: S.activation(T.fw[:, 512 * k:512 * k + 512], T.eighth[:], F.Copy, scale=0.0), "c8")
    const("off", lambda: S.activation(T.off[:], T.c0[:], F.Abs, bias=T.pi[:]), "c0", "pi")
    const("maskb", lambda: S.activation(T.maskb[:], T.off[:], F.Copy, scale=-2.0 * BIG, bias=BIG), "off")
    const("hold", lambda: S.activation(T.hold[:], T.c0[:], F.Sign), "c0")
    const("urs", lambda: S.activation(T.urs[:, 0:128], T.us[:, 0:128].indirect(T.uoff[:, 0:8]), F.Copy), "uq", "uoff")
    const("dja", lambda: S.activation(T.dja[:], T.dj[:], F.Abs), "dj")
    for j in range(4):
        w = PK if j % 2 else 1.0
        const("fw%d" % j, lambda j=j, w=w: S.activation(T.fw[:, 512 * (j // 2) + j:512 * (j // 2) + 512:4], T.dja[:], F.Relu, scale=-w, bias=w), "dja", "fw0%d" % (j // 2))

    ow = owners(T, topo)
    own = ow.index(rank)
    mate = [r for r in range(len(T.cores)) if r != rank and topo.chip(T.cores[r]) == topo.chip(core)]
    far = [r for r in range(len(T.cores)) if topo.chip(T.cores[r]) != topo.chip(core)]
    fe = topo.engines(core, T.cores[far[0]])
    pairs = [fe[2 * k:2 * k + 2] for k in range(4)]
    ne = [e for e in topo.engines(core, T.cores[mate[0]]) if e not in fe][:2]
    local = [0]

    def put(src, rs, dst, sm, es):
        ids = []
        for r in rs:
            rid, pid, _se = topo.addr(T.cores[r])
            ids.append(DstId(rid=rid, pnc=pid))
        local[0] += len(es)
        return RemoteDMATransfer(dst_ids=ids, dma_engine_mask=sum(1 << e for e in es), remote_sem=sem[sm], srcs=[src], dsts=[dst] * len(rs))

    TURN = [([0, 1, 2], [3, 0, 1]), ([3, 2, 0], [1, 2, 3])]
    BANK = [(T.pa, 0), (T.pa, 512), (T.pa, 1024), (T.pa, 1536), (T.pe, 0)]

    def pick(q, k, name, out, window, lst, scale, *ready):
        b, a, e = [int(z) for z in k[1:].split("_")]
        o, w = out[:, 64 * a + b:64 * e:4], window[:, 512 * b:512 * b + 512].indirect(lst[:, a:e])
        if q == "s": s(name, lambda: S.activation(o, w, F.Copy, scale=scale), *ready)
        elif scale == 1.0: v(name, lambda: V.tensor_copy(o, w), *ready)
        else: v(name, lambda: V.tensor_scalar(o, w, scale, None, A.mult), *ready)

    def covering(plan, t, letter, a, e):
        return ["%s@%d" % (k, t) for q in "vs" for k in plan[q].split() if k[0] == letter and int(k.split("_")[1]) < e and int(k.split("_")[2]) > a]

    def head(q, k, t):
        b = int(k[1])
        if k[0] == "w":
            c, a = [T.pp, T.pc, T.pe, T.pf][b], 512 * b + 256
            v("%s@%d" % (k, t), lambda: V.tensor_tensor(T.sn[:, a:a + 256], c[:, 0:256], T.sh[:, 1024 + b:2048:4], A.add), "d1%d@%d" % (b, t - 1))
        else: pick(q, k, "%s@%d" % (k, t), T["x%d" % t], T.sn, T.il, 4.0, "w%d@%d" % (b, t))

    def one_round(t):
        X, XP = T["x%d" % t], T["xp%d" % t]
        XQ, XS = T["xq%d" % t], T["xs%d" % t]
        SQ, SS, LC, LS = T["sq%d" % t], T["ss%d" % t], T["lc%d" % t], T["ls%d" % t]
        HQ, HS, HL, HP = T["hq%d" % t], T["hs%d" % t], T["hl%d" % t], T["hp%d" % t]
        last = t == R - 1
        plan = PLAN[t]
        N = lambda k: "%s@%d" % (k, t)
        vs, ss, ps = plan["v"].split(), plan["s"].split(), plan["p"].split()
        lo, hi = plan["pairs"]
        nw = (hi - lo) // 2 + 1
        have = [covering(plan, t, "x", 0, 16), covering(plan, t, "x", 16, 32)] if t else [[("lxa", 16)], [("lxb", 16)]]
        sums = [N("odd")] + [N(k) for k in ss if k[0] == "d"]
        signs = [k for k in ss if k[0] == "s"]
        writer = {m: N(("r%d" if "r%d" % m in ss else "f%d") % m) for m in range(1, 32)}
        writer[32] = N("dg")
        folds = [int(k[1:]) for k in ps if k[0] == "o"]
        bank = {m: BANK[n % len(BANK)] for n, m in enumerate(folds)}
        before = {m: N("a%d" % folds[n - len(BANK)]) for n, m in enumerate(folds) if n >= len(BANK)}
        tiles = [int(k[1:]) for k in ps if k[0] == "c"]
        early = [k for k in vs[:vs.index("pmD")] if k[0] == "f" and k != "fq"]
        part = {"A": (0, 256, T.pp, "sA"), "D": (256, 512, T.pe, "sB")}
        held = lambda m: N("scA" if m < 16 else "scD")
        col = lambda m: T.sc[:, 16 * m + 15:16 * m + 16]
        rows = lambda m: T.ft[:, 4 * CO[slot(m)[0]] + slot(m)[1]:4 * CO[slot(m)[0]] + 64 * m:4]
        listed = lambda k: N("lo%d" % (int(k.split("_")[1]) // 16))
        for b in range(4):
            gg(N("xp"), lambda b=b: g.affine_select(XP[:, 512 * b:512 * b + 512], X[:, b:2048:4], [[0, 512]], A.is_ge, 0.0, 0, 0), *(have[0] + have[1]))
        for b in range(4 if t == 0 else 0):
            gg("eb", lambda b=b: g.affine_select(T.eb[:, 512 * b:512 * b + 512], T.eighth[:], [[-1, 512]], A.is_equal, 0.0, b, 4), "c8")
        for k in vs:
            if k[0] == "_": v(k[1:], K[k[1:]][0], *K[k[1:]][1])
            elif k[0] in "wx": head("v", k, t)
            elif k[0] == "t": pick("v", k, N(k), T.st, XP, T.lo, 1.0, listed(k), N("xp"))
            elif k == "e1": v(N(k), lambda: V.tensor_tensor_scan(T.e1[:], T.hk[:], T.pc[:], 0.0, A.mult, A.max), N("c%d" % tiles[-1]), "hk")
            elif k == "a2": v(N(k), lambda: V.tensor_tensor(T.a2[:], T.a1[:], T.cr[:], A.add), N("a1"), N("cr"))
            elif k == "a2b": v(N(k), lambda: V.tensor_tensor(T.a2b[:], T.a2[:], T.e1[:, 15:512:16], A.add), N("a2"), N("e1"))
            elif k == "a3": v(N(k), lambda: V.tensor_tensor(T.a3[:], T.a2b[:], T.rs[:], A.subtract), N("a2b"), *sums)
            elif k == "il": v(N(k), lambda: V.tensor_copy(T.il[:], T.a3[:]), N("a3"))
            elif k == "inv": v(N(k), lambda: V.tensor_copy(T.inv[:, 0:512].indirect(T.il[:, 0:32]), T.iot[:]), N("il"), "iot")
            elif k[:2] == "e2":
                h = int(k[2])
                v(N(k), lambda h=h: V.tensor_tensor_scan(T.e2[:, 256 * h:256 * h + 256], T.hk[:, 0:256], T.inv[:, 256 * h:256 * h + 256], 0.0, A.mult, A.max), N("inv"))
            elif k[:2] == "lo":
                h = int(k[2])
                v(N(k), lambda h=h: V.tensor_scalar(T.lo[:, 16 * h:16 * h + 16], T.e2[:, 256 * h + 15:256 * h + 256:16], T.isc[:], -1.0, A.mult, A.add), N("e2%d" % h), "isc")
            elif k[:2] == "sq":
                h = int(k[2])
                v(N(k), lambda h=h: V.quantize_mx(SQ[:, 256 * h:256 * h + 256], SS[:, 256 * h:256 * h + 256], T.st[:, 1024 * h:1024 * h + 1024]),
                  *covering(plan, t, "t", 16 * h, 16 * h + 16))
            elif k in ("qA", "qB"):
                h = "AB".index(k[1])
                v(N(k), lambda h=h: V.quantize_mx(XQ[:, 256 * h:256 * h + 256], XS[:, 256 * h:256 * h + 256], X[:, 1024 * h:1024 * h + 1024]), *have[h])
            elif k == "fq":
                v("fq", lambda: V.quantize_mx(T.fwq[:], T.fws[:], T.fw[:]), "fw0", "fw1", "fw2", "fw3")
            elif k[:2] == "pm":
                a, e, q, d = part[k[2]]
                v(N(k), lambda a=a, e=e, q=q: V.tensor_tensor(T.pm[:, a:e], q[:, 0:256], T.maskb[:, a:e], A.min), N(d), "maskb")
            elif k[:2] == "sc":
                a, e = part[k[2]][:2]
                v(N(k), lambda a=a, e=e: V.tensor_tensor_scan(T.sc[:, a:e], T.rst[:, a:e], T.pm[:, a:e], -BIG, A.min, A.max), N("pm" + k[2]), "rst")
            elif k == "dg":
                v(N(k), lambda: V.tensor_tensor(T.ft[:, 0:4 * C:4], T.pp[:], T.sc[:], A.is_le), N("sZ"), N("scA"), N("scD"), "z0")
            elif k == "cum":
                v(N(k), lambda: V.tensor_tensor_scan(T.cum[:], T.hold[:], T.ft[:, 0:4 * C:4], 0.0, A.mult, A.add), N("dg"), "hold")
            elif k == "bq":
                v("bq", lambda: V.quantize_mx(T.bq[:], T.bs[:], T.bt[:]), "b1")
            elif k == "a1":
                v(N(k), lambda: V.tensor_tensor(T.a1[:], T.ac0[:], T.cum[:, 15:512:16], A.subtract), N("cum"), "ac0")
            elif k[0] == "f":
                m = int(k[1:])
                v(N(k), lambda m=m: V.tensor_scalar(rows(m), T.pp[:, 0:16 * m], col(m), None, A.is_lt), N("sA" if k in early else "sZ"), held(m), "z%d" % slot(m)[0])
            else:
                i = int(k[1:])
                a, e = CO[i], CO[i] + NS[i]
                v(N(k), lambda a=a, e=e: V.quantize_mx(T.fq[:, a:e], T.fs[:, a:e], T.ft[:, 4 * a:4 * e]), *[writer[32 - 4 * i - j] for j in range(4)])
        for k in ss:
            m = int(k[1:]) if k[0] in "srad" else 0
            if k[0] == "_": s(k[1:], K[k[1:]][0], *K[k[1:]][1])
            elif k[0] == "x": head("s", k, t)
            elif k[0] == "t": pick("s", k, N(k), T.st, XP, T.lo, 1.0, listed(k), N("xp"))
            elif k == "hk":
                s("hk", lambda: S.activation(T.hk[:], T.hk1[:, 0:16].indirect(T.rep[:, 0:32]), F.Copy), "hk1", "rep")
            elif k == "hw":
                s(N("hw"), lambda: S.activation(T.hw[:, 0:nw], T.rs[:, lo:hi + 1:2], F.Copy, scale=1.0 / PK, bias=WHOLE), *[N("a%d" % m) for m in folds])
                s(N("cr"), lambda: S.activation(T.cr[:, lo:hi + 1:2], T.hw[:, 0:nw], F.Copy, scale=PK, bias=-WHOLE * PK), N("hw"), "cr0")
                s(N("odd"), lambda: S.activation(T.rs[:, lo - 1:hi:2], T.hw[:, 0:nw], F.Copy, bias=-WHOLE))
            elif k[0] == "s":
                o = 512 * signs.index(k)
                src = T.pa[:, 1536:1536 + 16 * m] if m < 16 else T.pf[:, 0:16 * m]
                s(N(k), lambda m=m, o=o, src=src: S.activation(T.sg[:, o:o + 16 * m], src, F.Sign, scale=-1.0, bias=col(m)), N("sX" if m < 16 else "sY"), held(m))
            elif k[0] == "r":
                o = 512 * signs.index("s%d" % m)
                s(N(k), lambda m=m, o=o: S.activation(rows(m), T.sg[:, o:o + 16 * m], F.Relu, accum_out=T.rs[:, m:m + 1]), N("s%d" % m), "z%d" % slot(m)[0], "rs0")
            elif k[0] == "a":
                q, c = bank[m]
                w = min(FOLD[slot(m)[0]], 16 * m)
                jo = 112 * m
                s(N(k), lambda m=m, q=q, c=c, w=w, jo=jo: S.activation(T.junk[:, jo:jo + w], q[:, c:c + w], F.Copy, accum_out=T.rs[:, m:m + 1]), N("o%d" % m), "rs0")
            else:
                s(N(k), lambda m=m: S.activation(T.junk[:, 128 * m - 128:144 * m - 128], rows(m), F.Copy, accum_out=T.rs[:, m:m + 1]), N("f%d" % m), "rs0")
        for k in ps:
            if k[0] == "s":
                o, a, e, d = {"A": (T.pp[:, 0:256], 0, 256, [N("qA")]), "B": (T.pe[:, 0:256], 256, 512, [N("qB")]), "X": (T.pa[:, 1536:1792], 0, 256, [N("qA")]),
                              "Y": (T.pf[:], 0, 512, [N("qA"), N("qB")]), "Z": (T.pp[:], 0, 512, [N("qB"), N("pmA")] + [N(f) for f in early])}[k[1]]
                p(N(k), lambda o=o, a=a, e=e: P.matmul_mx(o, T.ur[:], T.urs[:], XQ[:, a:e], XS[:, a:e], True, True), "ur", "urs", *d)
            elif k[0] == "o":
                m = int(k[1:])
                i, j = slot(m)
                q, c = bank[m]
                w = FOLD[i]
                n = -(-16 * m // w)
                d = [N("q%d" % i), "fq", N("pmD")] + ([before[m]] if m in before else [])
                d += [N(z) for z in signs if int(z[1:]) < 16 and c == 1536]
                for e in range(n):
                    a = CO[i] + w * e
                    p(N(k), lambda q=q, c=c, w=w, a=a, e=e, n=n, j=j: P.matmul_mx(q[:, c:c + w], T.fwq[:, 64 * j:64 * j + 128], T.fws[:, 64 * j:64 * j + 128],
                                                                                T.fq[:, a:a + w], T.fs[:, a:a + w], e == 0, e == n - 1), *d)
            else:
                i = int(k[1:])
                p(N(k), lambda i=i: P.matmul_mx(T.pc[:, 0:NS[i]], T.bq[:], T.bs[:], T.fq[:, CO[i]:CO[i] + NS[i]], T.fs[:, CO[i]:CO[i] + NS[i]], i == tiles[0], i == tiles[-1]),
                  N("q%d" % i), "bq")
        for h in range(2):
            d_q = N("sq%d" % h)
            blocks = [4 * h + k for k in range(4)]
            for kind in range(2):
                tr, k = [], 0
                for b in blocks:
                    r = ow[b]
                    if r == rank: continue
                    if r in mate: es = ne
                    else:
                        es = pairs[TURN[h][kind][k]]
                        k += 1
                    if kind == 0: sv, dv = SQ[:, BL * b:BL * b + BL].bitcast(dt.uint8), LC[:, BL * rank:BL * rank + BL].bitcast(dt.uint8)
                    else: sv, dv = SS[:, BL * b:BL * b + BL], LS[:, BL * rank:BL * rank + BL]
                    tr.append(put(sv, [r], dv, "sa%d_%d" % (t, rank), es))
                raw("g", lambda tr=tr: g.remote_dma_fused(tr, local_sem=sem.lsem), d_q)
            if own in blocks:
                raw("y", lambda: Y.dma_start(LC[:, BL * rank:BL * rank + BL].bitcast(dt.uint8), SQ[:, BL * own:BL * own + BL].bitcast(dt.uint8)).then_inc(sem["cs%d" % t], 16), d_q)
                raw("y", lambda: Y.dma_start(LS[:, BL * rank:BL * rank + BL], SS[:, BL * own:BL * own + BL]).then_inc(sem["cs%d" % t], 16))
        if t == 0:
            v("eq", lambda: V.quantize_mx(T.eq[:], T.es[:], T.eb[:]), "eb")
            v("mt", lambda: V.memset(T.mt[:], 0.0))
            v("ht", lambda: V.memset(T.ht[:], 0.0))
            for w in range(R): v("pad", lambda w=w: V.quantize_mx(T["lc%d" % w][:, 512:640], T["ls%d" % w][:, 512:640], T.mt[:]), "mt")
        v(N("sh"), lambda: V.tensor_scalar(T.sh[:], T.st[:], 0.125, None, A.mult))
        if last:
            v("ol", lambda: V.tensor_scalar(T.olt[:], T.inv[:], -1.0, None, A.add))
            v("vq", lambda: V.quantize_mx(T.vq[:], T.vsc[:], T.vt[:]), ("lv", 16))
            raw("y", lambda: Y.dma_start(T.ol[:, :], T.olt[0:128:16, :]).then_inc(sem.so, 16), "ol")
        arrived = lambda r: ("cs%d" % t, 32) if r == rank else ("sa%d_%d" % (t, r), 2 * len(ne) if r in mate else 4)
        E = lambda b: (T.eq[:, 128 * b:128 * b + 128], T.es[:, 128 * b:128 * b + 128])
        wait = [d_q, "eq", "pad"] + [arrived(r) for r in range(8)]
        side = {b: q for b, q in zip(SIDE, (T.pp, T.pc))}
        for b in SIDE:
            p(N("u%d" % b), lambda b=b: P.matmul_mx(side[b][:, 0:C - BL * KP], *E(b), LC[:, BL * KP:C], LS[:, BL * KP:C], True, True), *wait)
            s(N("k%d" % b), lambda b=b: S.activation(T.acb[:, BL * b:BL * b + BL], side[b][:, 0:BL], F.Copy), N("u%d" % b))
        for b in list(SIDE) + [b for b in range(4) if b not in SIDE]:
            n = KP if b in SIDE else 8
            for r in range(n):
                p(N("m%d" % b), lambda r=r, b=b, n=n: P.matmul_mx(T.pa[:, 512 * b:512 * b + 128], *E(b), LC[:, BL * r:BL * r + 128], LS[:, BL * r:BL * r + 128], r == 0, r == n - 1), *wait)
        for r in range(KP, 8):
            for b in SIDE:
                x = T.pa[:, 512 * b:512 * b + BL] if r == KP else side[b][:, BL * (r - KP):BL * (r - KP + 1)]
                out = T.acb[:, BL * b:BL * b + BL] if r < 7 else T.mt[:, b:256:4]
                v(N("acc%d%d" % (r, b)), lambda x=x, out=out, b=b: V.tensor_tensor(out, x, T.acb[:, BL * b:BL * b + BL], A.add),
                  *([N("m%d" % b), N("k%d" % b), "mt"] if r == KP else [N("acc%d%d" % (r - 1, b))]))
        for b in range(4):
            if b not in SIDE: s(N("acc7%d" % b), lambda b=b: S.activation(T.mt[:, b:256:4], T.pa[:, 512 * b:512 * b + 64], F.Copy), N("m%d" % b), "mt")
        v(N("mq"), lambda: V.quantize_mx(T.mq[:], T.ms[:], T.mt[:]), *[N("acc7%d" % b) for b in range(4)])
        for b in range(4):
            p(N("h%d" % b), lambda b=b: P.matmul_mx(T.pa[:, 512 * b:512 * b + 128], T.wq[:, 128 * b:128 * b + 128], T.wsc[:, 128 * b:128 * b + 128], T.mq[:], T.ms[:], True, True),
              N("mq"), ("lw", 16), ("lws", 16))
            if b % 2 == 0: s(N("re%d" % b), lambda b=b: S.activation(T.ht[:, b:256:4], T.pa[:, 512 * b:512 * b + 64], F.Relu, scale=0.0625), N("h%d" % b), "ht")
            else: v(N("re%d" % b), lambda b=b: V.tensor_scalar(T.ht[:, b:256:4], T.pa[:, 512 * b:512 * b + 64], 0.0, 0.0625, A.max, A.mult), N("h%d" % b), "ht")
        d_hq = v(N("hq"), lambda: V.quantize_mx(HQ[:], HS[:], T.ht[:]), *[N("re%d" % b) for b in range(4)])
        hsem = ["ha%d" % t, "hb%d" % t]
        for kind in range(2):
            if kind == 0: sv, dv = HQ[:, 0:BL].bitcast(dt.uint8), HL[:, BL * own:BL * own + BL].bitcast(dt.uint8)
            else: sv, dv = HS[:, 0:BL], HP[:, BL * own:BL * own + BL]
            tr = [put(sv, far, dv, hsem[own // 4], fe), put(sv, mate, dv, hsem[own // 4], ne)]
            raw("g", lambda tr=tr: g.remote_dma_fused(tr, local_sem=sem.lsem), d_hq)
        raw("y", lambda: Y.dma_start(HL[:, BL * own:BL * own + BL].bitcast(dt.uint8), HQ[:, 0:BL].bitcast(dt.uint8)).then_inc(sem["ch%d" % t], 16), d_hq)
        raw("y", lambda: Y.dma_start(HP[:, BL * own:BL * own + BL], HS[:, 0:BL]).then_inc(sem["ch%d" % t], 16))
        for h in range(2):
            rs = [r for r in ow[4 * h:4 * h + 4] if r != rank]
            d = [d_hq, (hsem[h], 2 * sum(len(ne) if r in mate else len(fe) for r in rs))]
            if own // 4 == h: d.append(("ch%d" % t, 32))
            at = [(T.pa, 512 * b) for b in range(4)] if h == 0 else [(T.pp, 0), (T.pc, 0), (T.pe, 0), (T.pf, 0)]
            for b in range(4):
                q, c = at[b]
                p(N("d%d%d" % (h, b)), lambda q=q, c=c, b=b, h=h: P.matmul_mx(q[:, c:c + 256], *E(b), HL[:, 256 * h:256 * h + 256], HP[:, 256 * h:256 * h + 256], True, True), *d)
                if h == 0:
                    v(N("add%d" % b), lambda q=q, c=c, b=b: V.tensor_tensor(T.sn[:, 512 * b:512 * b + 256], q[:, c:c + 256], T.sh[:, b:1024:4], A.add), N("d0%d" % b), N("sh"))

    for t in range(R): one_round(t)
    plan = PLAN[R]
    XN, XQ2, XS2 = T["x%d" % R], T["xq%d" % R], T["xs%d" % R]
    cuts = plan["cuts"]
    n = len(cuts) - 1
    for q in "vs":
        for k in plan[q].split():
            if k[0] in "wx":
                head(q, k, R)
                continue
            j = int(k[1])
            a, e = 16 * cuts[j], 16 * cuts[j + 1]
            if k[0] == "q": v(k, lambda a=a, e=e: V.quantize_mx(XQ2[:, a:e], XS2[:, a:e], XN[:, 4 * a:4 * e]), *covering(plan, R, "x", cuts[j], cuts[j + 1]))
            elif k[0] == "y" and q == "s": s(k, lambda a=a, e=e, j=j: S.activation(T.yt[:, a:e], T.pa[:, 512 * j:512 * j + e - a], F.Copy), "py%d" % j)
            elif k[0] == "y": v(k, lambda a=a, e=e, j=j: V.tensor_copy(T.yt[:, a:e], T.pa[:, 512 * j:512 * j + e - a]), "py%d" % j)
            else: raw("s", lambda a=a, e=e: S.dma_start(T.y[:, a:e], T.yt[:, a:e]).then_inc(sem.so, 16), "y%d" % j)
    for j in range(n):
        a, e = 16 * cuts[j], 16 * cuts[j + 1]
        p("py%d" % j, lambda a=a, e=e, j=j: P.matmul_mx(T.pa[:, 512 * j:512 * j + e - a], T.vq[:], T.vsc[:], XQ2[:, a:e], XS2[:, a:e], True, True), "q%d" % j, "vq")
    for k in plan["y"].split():
        j = int(k[1])
        if k[0] == "O":
            raw("y", lambda j=j: Y.dma_start(T.osc[4 * j:4 * j + 4, :], XS2[32 * j:32 * j + 4, :]).then_inc(sem.so, 16), "q%d" % (n - 1))
            continue
        a, e = 16 * cuts[j], 16 * cuts[j + 1]
        if k[0] == "C": raw("y", lambda a=a, e=e: Y.dma_start(T.oc[:, 4 * a:4 * e], XQ2[:, a:e].bitcast(dt.uint8)).then_inc(sem.so, 16), "q%d" % j)
        else: raw("y", lambda a=a, e=e: Y.dma_start(T.y[:, a:e], T.yt[:, a:e]).then_inc(sem.so, 16), "y%d" % j)
    raw("g", None, ("lsem", local[0]))
    raw("y", None, ("so", 16 * (2 * n + 5)), *[(SEM[q], count[q]) for q in SEM])

    for q in Q:
        seen = {}
        for fn, deps, counted in calls[q]:
            for d in deps:
                k, n = named[d] if isinstance(d, str) else d
                if seen.get(k, 0) < n:
                    Q[q].wait_ge(sem[k], n)
                    seen[k] = n
            if fn is None: continue
            inst = fn()
            if counted: inst.then_inc(sem[SEM[q]], 1)
